import numpy as np, ml_dtypes
CORES = [25,29,65,69,153,157,193,197]
N = 8
import mx_ref
BF = ml_dtypes.bfloat16
def pick(q, e):
    c = np.concatenate([q[0].reshape(128, -1, 4), np.zeros((128, 1, 4), np.uint8)], axis=1); s = np.concatenate([q[1], np.ones((16, 1), np.uint8)], axis=1)
    return (np.ascontiguousarray(c[:, e].reshape(128, -1)), np.ascontiguousarray(s[:, e]))
def join(*qs):
    return (np.concatenate([q[0] for q in qs], axis=1), np.concatenate([q[1] for q in qs], axis=1))
def put(q, e, v):
    c, s = q[0].reshape(128, -1, 4).copy(), q[1].copy(); c[:, e] = v[0].reshape(128, -1, 4); s[:, e] = v[1]
    return (c.reshape(128, -1), s)
def pk(c, s):
    return (np.ascontiguousarray(c), mx_ref.live(s))
def emit(q):
    return q[0], q[1]
def cut(t, i, w=512):
    return t[:, w * i:w * i + w]
def f(rng, *shape):
    return mx_ref.flush((rng.standard_normal(shape, dtype=np.float32) * np.exp2(rng.integers(-2, 3, shape[:-1] + (1,)))).astype(BF))
def wide(rng, *shape, cols=0):
    v = rng.standard_normal(shape, dtype=np.float32) * np.exp2(rng.integers(-12, 13, shape)).astype(np.float32)
    if cols: v *= np.repeat(np.exp2(rng.integers(-cols, cols + 1, shape[:-2] + (1, shape[-1] // 4))) * (rng.random(shape[:-2] + (1, shape[-1] // 4)) > 0.0625), 4, axis=-1).astype(np.float32)
    return mx_ref.flush(v.astype(BF))
P, CAPP, O, L, S = 128, 32, 1, 3, 128
def plain(rng):
    v = np.array(f(rng, 128, 512))
    v[:, 4 * L:] = 0
    return {"x": f(rng, N, 128, 4 * P), "pl": np.stack([v] * N), "w": f(rng, N, 128, 512 * O)}
def sized(rng, *shape):
    return (1 + rng.random(shape)) * rng.choice([-1.0, 1.0], shape)
def planes(rng):
    v = np.zeros((128, 128, 4))
    for b in range(L): v[8 * b:8 * b + 8, b] = sized(rng, 8, 4)
    return np.stack([v.reshape(128, 512)] * N).astype(np.float32).astype(BF)
def aim(v, t, pl):
    for b in range(L):
        g = np.sign(pl[0].astype(np.float32).reshape(128, 128, 4)[8 * b:8 * b + 8, b])
        v[:, 8 * b:8 * b + 8] = np.abs(v[:, 8 * b:8 * b + 8]) * g[None, :, None, :] * (1 - 2 * (t >> b & 1))[:, None, :, None]
    return v.reshape(N, 128, 4 * P).astype(np.float32).astype(BF)
def setup_inputs(rng):
    d = plain(rng)
    v = d["x"].astype(np.float32).reshape(N, 128, P, 4).transpose(1, 0, 2, 3).reshape(128, N * P, 4)
    e, n = rng.permutation(N * P), N * P // 4
    near, of = e[:n], rng.choice(e[n:], n)
    size, change = np.exp2(rng.integers(-1, 2, (n, 1))), rng.choice([0.0, 0.0625, 0.25, 0.5], (n, 1))
    v[:, near] = v[:, of] * size * (1 + change * rng.standard_normal((128, n, 4)))
    d["x"] = mx_ref.flush(v.reshape(128, N, P, 4).transpose(1, 0, 2, 3).reshape(N, 128, 4 * P).astype(BF))
    return d
def setup_inputs_same(rng):
    d, first = plain(rng), rng.permutation(N)
    if first[0] == 0: first[0], first[1] = int(first[1]), int(first[0])
    d["pl"], u = planes(rng), sized(rng, 128, N, 4)
    t = np.stack([rng.permutation(np.flatnonzero(first <= s)[np.arange(P) % (s + 1)]) for s in range(N)])
    v = np.stack([u[:, t[s]] for s in range(N)])
    v[first[0]][:, np.flatnonzero(t[first[0]] == 0)[::2]] = 0
    d["x"] = aim(v, t, d["pl"])
    return d
def setup_inputs_full(rng):
    d, h, r = plain(rng), rng.permutation(N), rng.permutation(N)
    n = rng.integers(CAPP + 1, 2 * CAPP + 1, N)
    n[r[0]] = CAPP
    n[r[1]] = P
    t = np.stack([rng.permutation(np.concatenate([np.full(n[s], h[0]), rng.choice(h[2:], P - n[s])])) for s in range(N)])
    d["pl"] = planes(rng)
    d["x"] = aim(sized(rng, N, 128, P, 4), t, d["pl"])
    return d
def setup_inputs_edge(rng):
    d, n = plain(rng), N * P // 4
    o = np.stack([s * P + rng.permutation(P) for s in range(N)]).reshape(N, P // 4, 4)
    m = np.sort(np.concatenate([rng.permutation(o[:, k].reshape(-1)).reshape(N, 4) for k in range(P // 4)]), axis=1)
    v = np.repeat(rng.choice([-1.0, 1.0], (n, 1, 512)), 4, axis=1)
    e, k = 32 * L + np.argsort(rng.random((n, 512 - 32 * L)), axis=1)[:, :49], np.arange(n)[:, None]
    v[k, 1, e[:, :16]] *= -1
    v[k, 2, e[:, :32]] *= -1
    v[k, 3, e[:, 32:]] *= -1
    x, t = np.zeros((N * P, 512)), np.zeros(N * P, int)
    x[m] = v * np.exp2(rng.integers(0, 2, (n, 1, 1)))
    x[m[0, 3]] = 0
    t[m] = np.repeat(np.arange(P // 4) % N, N)[:, None]
    d["pl"] = planes(rng)
    d["x"] = aim(np.ascontiguousarray(x.reshape(N, P, 128, 4).transpose(0, 2, 1, 3)), t.reshape(N, P), d["pl"])
    return d
def setup_inputs_deal(rng):
    d, t = plain(rng), []
    c = np.ones(N, int)
    c[0], c[N - 1] = 2, 0
    for s in range(N):
        a = np.bincount(rng.permutation(np.repeat(np.arange(N), (CAPP - c[s]) // N))[:P // N - c[s]], minlength=N)
        t.append(rng.permutation(np.repeat(np.arange(N), N * a + c[s])))
    d["pl"] = planes(rng)
    d["x"] = aim(sized(rng, N, 128, P, 4), np.stack(t), d["pl"])
    return d
def setup_inputs_spread(rng):
    d, x = plain(rng), np.array(wide(rng, N, 128, 4 * P, cols=6))
    x[0, :, :4] = -0.0
    d["pl"][:, :, :4] = np.abs(d["pl"][:, :, :4])
    return {**d, "x": x}
def check_inputs(d):
    b = []
    for k in ("x", "pl", "w"):
        v = np.abs(d[k].astype(np.float32))
        if not (np.isfinite(v).all() and ((v == 0) | (v >= 2.0 ** -30) & (v <= 2.0 ** 30)).all()): b.append("a value of " + k)
    v = d["pl"].astype(np.float32)
    if (v[:, :, 4 * L:] != 0).any(): b.append("pl has numbers behind its first L columns")
    if (v != v[:1]).any(): b.append("pl differs between ranks")
    return b
def reference(x, pl, w):
    q = [mx_ref.quantize(np.ascontiguousarray(x[s])) for s in range(N)]
    every = join(*q)
    bucket = []
    for s in range(N):
        z = mx_ref.matmul(mx_ref.quantize(np.ascontiguousarray(pl[s])), q[s])
        bucket.append(sum((z[b] < 0) * 2 ** b for b in range(L)))
    alive = []
    for d in range(N):
        e = np.concatenate([P * s + np.flatnonzero(bucket[s] == d)[:CAPP] for s in range(N)])
        if e.size == 0: continue
        at = np.concatenate([e, np.full(-e.size % 128, -1)])
        m = np.concatenate([mx_ref.matmul(pick(every, at[i:i + 128]), pick(every, at)) for i in range(0, at.size, 128)])
        falls = np.triu(m >= np.float32(0.9375) * np.diagonal(m), 1).any(axis=0)
        alive.append(e[~falls[:e.size]])
    alive = np.concatenate(alive)
    oc, osc = np.zeros((N, 128, 4 * S), np.uint8), np.zeros((N, 16, S), np.uint8)
    num, y = np.zeros((N, 1, S), np.float32), np.zeros((N, 128, O * S), np.float32)
    for r in range(N):
        e = alive[r::N]
        e = np.concatenate([e, np.full(S - e.size, -1)])
        v = pick(every, e)
        oc[r], osc[r] = emit(v)
        num[r, 0] = e
        for o in range(O): y[r, :, o * S:o * S + S] = mx_ref.matmul(mx_ref.quantize(np.ascontiguousarray(cut(w[r], o))), v)
    return {"oc": oc, "osc": osc, "num": num, "y": y}

@@ -1,0 +1,412 @@
+from concourse.bass import DstId, RemoteDMATransfer
+from concourse.mybir import dt, AluOpType, AxisListType, ActivationFunctionType
+
+OP = AluOpType
+COPY = ActivationFunctionType.Copy
+IDENT = ActivationFunctionType.Identity
+SIGN = ActivationFunctionType.Sign
+X = AxisListType.X
+N, P, L, CAPP = 8, 128, 3, 32
+BIG = 1.0e29
+
+SCRATCH = {}
+for _kind, _list in {
+    "bfloat16": "plh 512 xh 520 wh 512 rstb 384 rst2 512 one 32 bits 384 bs 384 mt 256 cu 256 cm 256 junk1 256 "
+                "tt 64 cum 256 cm2 512 su2 512 junk3 512 cl 64 rm2 1 m1 2 nl1 64 rm1 1 n8 8",
+    "float8_e4m3fn_x4": "plc 128 prc 384 xq 130 wq 128 slot1c 256 land1c 256 ccc 256 slot3c 256 land3c 258 fq 128 r1c 64 r3c 64",
+    "uint8": "pls 128 prs 384 xs 130 ws 128 slot1s 256 land1s 256 ccs 256 slot3s 256 land3s 258 fs 128 r1s 64 r3s 64",
+    "uint16": "ofp 24 off1 16 offc 16 off3 20 nl3 64 m3 2 offz 8 rm3 1",
+    "int32": "pb 4 vi 10 v7 10 xi 8 xsh 8",
+    "float32": "rst9 72 pbf 4 nx 1 off 24 c32 64 ccr 256 c128 8 rhc 4 rh 4 bi 4 rq 4 bq 4 ggc 8 gg 8 k8 2 dm0 128 dm 128 cp 2 tri 384 "
+               "rc 10 dq 2 acc1 2 la1 2 em 8 ep 8 k0 1 ab 64 ab1 64 ab2 64 pd 256 junk2 256 thr 2 xg 384 nb 256 nt 256 "
+               "nw 256 acc2 2 nq 4 na 16 nwc 256 end 8 n3 64 nt3 64 d256 8 it 72 its 72 nf 256 nft 264 no 128 ysb 128",
+}.items():
+    _w = _list.split()
+    for _i in range(0, len(_w), 2):
+        SCRATCH[_w[_i]] = ("sbuf", [128, int(_w[_i + 1])], _kind)
+for _n in ("z0", "z1", "z2", "ga", "gb", "yp"):
+    SCRATCH[_n] = ("psum", [128, 512], "float32")
+SCRATCH["tw"] = ("sbuf", [128, 2, 32], "bfloat16")
+SCRATCH["bc"] = ("sbuf", [128, 2, 128], "bfloat16")
+SCRATCH["lq"] = ("sbuf", [128, 2, 2], "float32")
+SCRATCH["la"] = ("sbuf", [128, 2, 8], "float32")
+SEMAPHORES = ["qv", "qs", "qt", "qp", "ldp", "ldx", "ldw", "ldz", "dout", "ls",
+              "a1", "n1", "c2", "a3", "n3", "rc1", "rs1", "rn1", "rn2", "rc3", "rs3", "rn3"]
+
+
+def wiring(T, topo):
+    cores = T.cores
+    same = [[r for r in range(N) if cores[r] in topo.cores_of(cores[s]) or topo.same_plane(cores[s], cores[r])] for s in range(N)]
+    cross = [[r for r in range(N) if r not in same[s]] for s in range(N)]
+    relays = [[k for k in topo.cores_of(c) if k not in cores and topo.die(k) == topo.die(c)
+               and all(topo.may_write(k, cores[r]) for r in cross[s])][:2] for s, c in enumerate(cores)]
+    return same, cross, relays
+
+
+def eng(topo, src, dst, a, b):
+    return sum(1 << e for e in topo.engines(src, dst)[a:b])
+
+
+def dest(topo, src, dst):
+    rid, pid = topo.addr(dst, src)
+    return DstId(rid=rid, pnc=pid)
+
+
+HAND = ((0, 8), (8, 16))
+COL = {"peer": (8, 16), 0: (0, 4), 1: (4, 8)}
+MSG = {"relay": (8, 16), "far": (0, 8), "peer": (8, 16)}
+
+
+def view(T, buf, a, b):
+    v = T[buf][:, a:b]
+    return v.bitcast(dt.uint8) if buf[-1] == "c" else v
+
+
+def relay_program(g, core, T, topo, s, group):
+    to = [T.cores[r] for r in group]
+    sent = [0]
+
+    def go(sem, tr):
+        g.wait_ge(T.sem[sem], 8)
+        g.remote_dma_fused(tr, local_sem=T.sem.ls)
+        sent[0] += 8
+
+    def cols(sem, buf, land, rsem):
+        at = 32 * s
+        go(sem, [RemoteDMATransfer(dst_ids=[dest(topo, core, d)], dma_engine_mask=eng(topo, core, d, 4 * i, 4 * i + 4), remote_sem=T.sem[rsem],
+                                   src=view(T, buf, 32 * i, 32 * i + 32), dst=view(T, land, at, at + 32)) for i, d in enumerate(to)])
+
+    def note(sem, src, land, rsem):
+        go(sem, [RemoteDMATransfer(dst_ids=[dest(topo, core, d) for d in to], dma_engine_mask=eng(topo, core, to[0], 0, 8), remote_sem=T.sem[rsem],
+                                   srcs=[T[src][:]], dsts=[T[land][:, 8 * s:8 * s + 1]] * 2)])
+
+    note("rn1", "rm1", "nl1", "n1")
+    cols("rc1", "r1c", "land1c", "a1")
+    cols("rs1", "r1s", "land1s", "a1")
+    note("rn2", "rm2", "cl", "c2")
+    cols("rc3", "r3c", "land3c", "a3")
+    cols("rs3", "r3s", "land3s", "a3")
+    note("rn3", "rm3", "nl3", "n3")
+    g.wait_ge(T.sem.ls, sent[0])
+
+
+def rank_program(g, core, T, topo):
+    same_all, cross_all, relays_all = wiring(T, topo)
+    me = T.rank_of(core)
+    if me is None:
+        for s in range(N):
+            if core in relays_all[s]:
+                i = relays_all[s].index(core)
+                relay_program(g, core, T, topo, s, cross_all[s][2 * i:2 * i + 2])
+        return
+    same, cross, relays = same_all[me], cross_all[me], relays_all[me]
+    pos = cross + same
+    am = same.index(me)
+    peer = [r for r in same if r != me and T.cores[r] in topo.cores_of(core)]
+    far = [r for r in same if r != me and r not in peer]
+    ncol = 8 * len(peer) + 4 * len(far) + 4 * len(cross)
+    nmsg = 8 * (N - 1)
+
+    V, S, E, Y = g.vector, g.scalar, g.tensor, g.sync
+    Q = {"v": V, "s": S, "t": E, "p": g, "y": Y}
+    cnt, seen = {}, {}
+
+    def wait(q, deps):
+        best = {}
+        for s, v in deps:
+            best[s] = max(best.get(s, 0), v)
+        for s, v in best.items():
+            if seen.get((q, s), 0) < v:
+                Q[q].wait_ge(T.sem[s], v)
+                seen[(q, s)] = v
+
+    def do(q, call, *deps):
+        wait(q, deps)
+        name = "q" + q
+        cnt[name] = cnt.get(name, 0) + 1
+        call().then_inc(T.sem[name], 1)
+        return (name, cnt[name])
+
+    def load(q, sem, out, in_, *deps):
+        wait(q, deps)
+        cnt[sem] = cnt.get(sem, 0) + 16
+        Q[q].dma_start(out, in_).then_inc(T.sem[sem], 16)
+        return (sem, cnt[sem])
+
+    def vset(ap, c, *deps):
+        return do("v", lambda: V.memset(ap, c), *deps)
+
+    def ts(out, in0, s1, s2, op0, op1, *deps):
+        if op1 is None:
+            return do("v", lambda: V.tensor_scalar(out, in0, s1, None, op0), *deps)
+        return do("v", lambda: V.tensor_scalar(out, in0, s1, s2, op0, op1), *deps)
+
+    def tt(out, a, b, op, *deps):
+        return do("v", lambda: V.tensor_tensor(out, a, b, op), *deps)
+
+    def vcopy(out, in_, *deps):
+        return do("v", lambda: V.tensor_copy(out, in_), *deps)
+
+    def red(out, in_, op, *deps):
+        return do("v", lambda: V.tensor_reduce(out, in_, X, op), *deps)
+
+    def scan(out, d0, d1, *deps, init=0.0, op1=OP.add):
+        return do("v", lambda: V.tensor_tensor_scan(out, d0, d1, init, OP.mult, op1), *deps)
+
+    def runs(out, in_, *deps):
+        return do("v", lambda: V.tensor_tensor_scan(out, in_, in_, 0.0, OP.add, OP.max), *deps)
+
+    def turn(out, in_, *deps):
+        return do("v", lambda: V.transpose(out, in_), *deps)
+
+    def act(out, in_, *deps):
+        return do("s", lambda: S.activation(out, in_, COPY), *deps)
+
+    def affine(out, in_, scale, bias, *deps):
+        return do("s", lambda: S.activation(out, in_, IDENT, bias, scale), *deps)
+
+    def count_s(out, junk, in_, bias, *deps):
+        return do("s", lambda: S.activation(junk, in_, SIGN, bias, -1.0, accum_out=out), *deps)
+
+    def iota(ap, pattern, base, cm=0, flag=True):
+        last = ("qp", cnt.get("qp", 0))
+        if flag:
+            return do("p", lambda: g.iota(ap, pattern, base, cm, allow_small_or_imprecise_dtypes=True), last)
+        return do("p", lambda: g.iota(ap, pattern, base, cm), last)
+
+    def spread(ns, out, in_, half, *deps):
+        for k in range(8):
+            a, b = k // 2, k // 2 ^ k % 2
+            if k * ns % 8 < ns:
+                hs = act(out(b, a), in_(a), *deps)
+            else:
+                hv = vcopy(out(b, a), in_(a), *deps)
+        return vcopy(half(1, 0), half(0, 0), hv, hs), act(half(0, 1), half(1, 1), hv, hs)
+
+    def quad(t, a, *cols):
+        return T[t][(slice(32 * a, 32 * a + 32),) + cols]
+
+    def pickc(out, win, off, *deps):
+        return do("v", lambda: V.tensor_copy(out.bitcast(dt.uint32), win.bitcast(dt.uint32).indirect(off)), *deps)
+
+    def pick(dst, src, n, a, b, off, *deps):
+        return (pickc(T[dst + "c"][:, a:b], T[src[0]][:, 0:n], off, *deps), act(T[dst + "s"][:, a:b], T[src[1]][:, 0:n].indirect(off), *deps))
+
+    def send(tr, *deps):
+        wait("p", deps)
+        g.remote_dma_fused([t for t, n in tr], local_sem=T.sem.ls)
+        cnt["ls"] = cnt.get("ls", 0) + sum(n for t, n in tr)
+
+    def xfer(src, dst, to, ab, sem):
+        return (RemoteDMATransfer(dst_ids=[dest(topo, core, c) for c in to], dma_engine_mask=eng(topo, core, to[0], ab[0], ab[1]),
+                                  remote_sem=T.sem[sem], srcs=[src], dsts=[dst] * len(to)), ab[1] - ab[0])
+
+    def send_cross(buf, rbuf, sem, *deps):
+        send([xfer(view(T, buf, 64 * i, 64 * i + 64), view(T, rbuf, 0, 64), [k], HAND[i], sem) for i, k in enumerate(relays)], *deps)
+
+    def send_same(buf, land, sem, *deps):
+        tr, at = [], 32 * me
+        for i, r in enumerate(far + peer):
+            a = 32 * pos.index(r)
+            tr.append(xfer(view(T, buf, a, a + 32), view(T, land, at, at + 32), [T.cores[r]], COL["peer" if r in peer else i], sem))
+        send(tr, *deps)
+
+    def note(src, land, sem, to, ab):
+        return xfer(src, T[land][:, 8 * me:8 * me + 1], [T.cores[r] for r in to], ab, sem)
+
+    def note_out(src, rbuf, rsem, *deps):
+        send([xfer(src[:, 0:1], T[rbuf][:], relays, MSG["relay"], rsem)], *deps)
+
+    def note_same(src, land, sem, *deps):
+        send([note(src, land, sem, far, MSG["far"]), note(src, land, sem, peer, MSG["peer"])], *deps)
+
+    ldp = load("y", "ldp", T.plh[:, 0:16], T.pl[:, 0:16])
+    ldx = load("s", "ldx", T.xh[:, 0:512], T.x[:])
+    ldw = load("y", "ldw", T.wh[:], T.w[:], ldx)
+    i_of = iota(T.off[:], [[1, L], [0, 8]], 0)
+    i_p = iota(T.pb[:, 0:1], [[1, 1]], 0, 1, False)
+    i_rh = iota(T.rhc[:], [[16, 4]], 0)
+    for a in range(4):
+        i_dq = iota(quad("dq", a, slice(0, 2)), [[pos[4 + a] - pos[a], 2]], pos[a])
+    iota(T.c128[:], [[128, 8]], 0)
+    iota(T.ggc[:], [[128, 8]], me)
+    iota(T.cp[:], [[128, 2]], 0, 1)
+    iota(T.c32[:], [[128, 2], [0, 32]], 0, 1)
+    i_cc = iota(T.ccr[:], [[-1, 256]], 255)
+    c_pl = vset(T.plh[:, 16:512], 0.0)
+    h = vset(T.rstb[:], 1.0)
+    c_of = vcopy(T.ofp[:], T.off[:], i_of)
+    c_x = vset(T.xh[:, 512:520], 0.0)
+    ts(T.pb[:, 1:2], T.pb[:, 0:1], 15, None, OP.bitwise_and, None, i_p)
+    ts(T.pb[:, 2:3], T.pb[:, 0:1], 4, 1, OP.logical_shift_right, OP.bitwise_and)
+    h2 = ts(T.pb[:, 3:4], T.pb[:, 0:1], 5, None, OP.logical_shift_right, None)
+    c_rb = vset(T.rstb[:, 0:384:3], 0.0, h)
+    c_pb = vcopy(T.pbf[:], T.pb[:], h2)
+    rho, p16, p32 = [T.pbf[:, i:i + 1] for i in (1, 2, 3)]
+    c_rh = affine(T.rh[:], T.rhc[:], 1.0, rho, c_pb, i_rh)
+
+    plq = do("v", lambda: V.quantize_mx(T.plc[:], T.pls[:], T.plh[:]), ldp, c_pl)
+    pr = []
+    for b in range(L):
+        w, o = slice(128 * b, 128 * b + 128), slice(8 * b, 8 * b + 8)
+        hv = pickc(T.prc[:, w], T.plc[:], T.ofp[:, o], plq, c_of)
+        pr.append((hv, act(T.prs[:, w], T.pls[:].indirect(T.ofp[:, o]), plq, c_of)))
+        if b == 0:
+            xq = do("v", lambda: V.quantize_mx(T.xq[:], T.xs[:], T.xh[:]), ldx, c_x)
+    ts(T.nx[:], p16, -1.0, 1.0, OP.mult, OP.add, c_pb)
+    c_bi = ts(T.bi[:], T.rhc[:], rho, 0.5, OP.add, OP.add, i_rh)
+    zs = [T.z0, T.z1, T.z2]
+    for b in range(L):
+        w = slice(128 * b, 128 * b + 128)
+        z = do("t", lambda: E.matmul_mx(zs[b][:, 0:128], T.prc[:, w], T.prs[:, w], T.xq[:, 0:128], T.xs[:, 0:128], True, True), xq, *pr[b])
+        h = ts(T.bits[:, b:384:3], zs[b][:, 0:128], 0.0, float(2 ** b), OP.is_lt, OP.mult, z)
+    bs = scan(T.bs[:], T.rstb[:], T.bits[:], h, c_rb)
+
+    XQ, L1, CC = ("xq", "xs"), ("land1c", "land1s"), ("ccc", "ccs")
+    w2 = [slice(128 * e, 128 * e + 128) for e in range(2)]
+    hm = [ts(T.mt[:, w], T.bs[:, 2:384:3], T.dq[:, e:e + 1], None, OP.is_equal, None, bs, i_dq) for e, w in enumerate(w2)]
+    cu = [runs(T.cu[:, w], T.mt[:, w], hm[e]) for e, w in enumerate(w2)]
+    hs = [count_s(T.acc1[:, e:e + 1], T.junk1[:, w], T.cu[:, w], T.bi[:, 1:2], cu[e], c_bi) for e, w in enumerate(w2)]
+    hc = [ts(T.cm[:, w], T.cu[:, w], T.rh[:, 0:1], None, OP.is_le, None, cu[e], c_rh) for e, w in enumerate(w2)]
+    h0 = [red(T.lq[:, e, 0:1], T.cm[:, w], OP.add, hc[e]) for e, w in enumerate(w2)]
+    hl = ts(T.la1[:], T.lq[:, :, 0], T.nx[:, 0:1], None, OP.mult, None, *h0)
+    for e in range(2):
+        lq = ts(T.lq[:, e, 1:2], T.acc1[:, e:e + 1], 0.5, 64.0, OP.mult, OP.add, hs[e])
+        m1 = affine(T.m1[:, e:e + 1], T.lq[:, e, 1:2], p16, T.la1[:, e:e + 1], lq, hl)
+        if e == 0:
+            note_out(T.m1, "rm1", "rn1", m1)
+    la = spread(3, lambda b, a: quad("la", b, slice(0, 2), slice(2 * a, 2 * a + 2)), lambda a: quad("lq", a, slice(0, 2), slice(0, 2)),
+                lambda b, a: T.la[64 * b:64 * b + 64, :, 4 * a:4 * a + 4], lq, *h0)
+    o0 = vcopy(T.off1[:, 0:8], T.la[:, 0, :], *la)
+    o1 = vcopy(T.off1[:, 8:16], T.la[:, 1, :])
+    pc, ps = pick("slot1", XQ, 130, 0, 128, T.off1[:, 0:8], o0, xq)
+    send_cross("slot1c", "r1c", "rc1", pc)
+    send_cross("slot1s", "r1s", "rs1", ps)
+    note_same(T.m1[:, 1:2], "nl1", "n1", m1)
+    pc, ps = pick("slot1", XQ, 130, 128, 256, T.off1[:, 8:16], o1, xq)
+    send_same("slot1c", "land1c", "a1", pc)
+    send_same("slot1s", "land1s", "a1", ps)
+    i = pos.index(me)
+    own1 = pick("land1", XQ, 130, 32 * me, 32 * me + 32, T.off1[:, 2 * i:2 * i + 2], o1, xq)
+    own_n = vcopy(T.nl1[:, 8 * me:8 * me + 1], T.m1[:, 1:2], m1)
+
+    load("y", "ldz", T.land3c[:, 256:258].bitcast(dt.uint8), T.xq[:, 128:130].bitcast(dt.uint8), xq)
+    ldz = load("y", "ldz", T.land3s[:, 256:258], T.xs[:, 128:130], xq)
+    c_nb = vset(T.nb[:], 0.0)
+    h = vset(T.dm0[:], 0.9375)
+    c_dm = do("p", lambda: g.affine_select(T.dm[:], T.dm0[:], [[-1, 128]], OP.is_equal, 0.0, 0, 1), h, i_cc)
+    for b in range(2):
+        w = 128 + 128 * b
+        c_tri = ts(T.tri[:, 128 * b:128 * b + w], T.ccr[:, 256 - w:256], T.cp[:, b:b + 1], BIG, OP.is_lt, OP.mult, i_cc)
+    c_one = vset(T.one[:], 1.0)
+    h = vset(T.rst2[:], 1.0)
+    c_r2 = vset(T.rst2[:, 0:512:256], 0.0, h)
+    h = vset(T.rst9[:], 1.0)
+    vset(T.rst9[:, 0:72:9], 0.0, h)
+    h = ts(T.k8[:, 0:1], p32, 64.0, rho, OP.mult, OP.add)
+    h = ts(T.rq[:], T.rhc[:], T.k8[:, 0:1], None, OP.add, None, h)
+    c_bq = ts(T.bq[:], T.rq[:], 0.5, None, OP.add, None, h)
+    h = ts(T.k8[:, 0:1], rho, 8.0, None, OP.mult, None, c_bq)
+    ts(T.k8[:, 1:2], T.k8[:, 0:1], 128.0, None, OP.add, None, h)
+    c_gg = ts(T.gg[:], T.ggc[:], T.k8[:, 0:1], None, OP.add, None, h)
+    vcopy(T.it[:, 0:72:9], T.gg[:], c_gg)
+    for i in range(N):
+        vset(T.rc[:, i:i + 1], 2048.0 + pos[i])
+    ts(T.rc[:, 8:10], T.dq[:], 2048.0, None, OP.add, None)
+    vset(T.nf[:], 0.0)
+    vset(T.nft[:, 256:264], -1.0)
+    c_all = do("v", lambda: V.quantize_mx(T.wq[:], T.ws[:], T.wh[:]), ldw)
+
+    a1, n1 = ("a1", 2 * ncol), ("n1", nmsg)
+    h = tt(T.nb[:, 0:256:32], T.nl1[:, 0:64:8], T.c128[:], OP.add, n1, own_n, c_nb, i_cc)
+    nt = turn(T.nt[:], T.nb[:], h)
+    n8 = do("p", lambda: g.partition_broadcast(T.n8[:], T.nl1[32 * am:32 * am + 1, 0:64:8], 128), n1, own_n, c_dm)
+    nw = do("p", lambda: g.partition_broadcast(T.nw[:], T.nt[32 * am:32 * am + 1, :], 128), nt, n8)
+    h = ts(T.em[:], T.n8[:], P - 1.0, None, OP.is_gt, None, n8)
+    h = scan(T.ep[:], T.em[:], T.one[:, 0:8], h, c_one, init=32.0, op1=OP.mult)
+    h = red(T.k0[:], T.ep[:], OP.add, h)
+    ts(T.ab1[:], T.c32[:], T.k0[:, 0:1], -2 * BIG, OP.is_equal, OP.mult, h)
+    h = ts(T.ab2[:], T.c32[:], T.k0[:, 0:1], 2 * BIG, OP.is_lt, OP.mult)
+    ab = tt(T.ab[:], T.ab1[:], T.ab2[:], OP.add, h)
+
+    gs, gm = [T.ga, T.gb], []
+    wd = [(slice(128 * b, 128 * b + 128), slice(128 * b, 128 + 256 * b), 128 + 128 * b) for b in range(2)]
+    for b in range(2):
+        w, w2, n = wd[b]
+        gm.append(do("t", lambda: E.matmul_mx(gs[b][:, 0:n], T.land1c[:, w], T.land1s[:, w], T.land1c[:, 0:n], T.land1s[:, 0:n], True, True), a1, *own1))
+    mx, th, hl, tr = [], [], [], []
+    for b in range(2):
+        w, w2, n = wd[b]
+        h = tt(T.pd[:, w], gs[b][:, w], T.dm[:], OP.mult, gm[b], c_dm)
+        th.append(do("s", lambda: S.activation(T.junk2[:, w], T.pd[:, w], COPY, accum_out=T.thr[:, b:b + 1]), h))
+        mx.append(do("v", lambda: V.tensor_tensor_scan(T.xg[:, w2], gs[b][:, n - 1::-1], T.tri[:, w2], 0.0, OP.max, OP.min), c_tri))
+    for b in range(2):
+        w = slice(32 * b, 32 * b + 32)
+        at = 128 * b + wd[b][2] - 1
+        hl.append(ts(T.tt[:, w], T.ab[:, w], T.xg[:, at:at + 1], T.thr[:, b:b + 1], OP.add, OP.is_lt, mx[b], th[b], ab))
+    for b in range(2):
+        tr.append(turn(T.tw[:, b, :], T.tt[:, 32 * b:32 * b + 32], hl[b]))
+    bc = spread(4, lambda b, a: quad("bc", b, slice(0, 2), slice(32 * a, 32 * a + 32)), lambda a: quad("tw", a, slice(0, 2), slice(0, 32)),
+                lambda b, a: T.bc[64 * b:64 * b + 64, :, 64 * a:64 * a + 64], *tr)
+    h = scan(T.cum[:, 0:128], T.rst2[:, 1:129], T.bc[:, 0, :], *bc)
+    cum = scan(T.cum[:, 128:256], T.rst2[:, 1:129], T.bc[:, 1, :], h, c_r2, init=T.cum[:, 127:128])
+
+    size = T.cum[:, 255:256]
+    send([xfer(size, T.rm2[:], [k], HAND[i], "rn2") for i, k in enumerate(relays)], cum)
+    note_same(size, "cl", "c2")
+    for c in range(2):
+        w = slice(256 * c, 256 * c + 256)
+        sa = count_s(T.acc2[:, c:c + 1], T.junk3[:, w], T.cum[:], T.bq[:, 2 + c:3 + c], cum, c_bq)
+        h = ts(T.cm2[:, w], T.cum[:], T.rq[:, c:c + 1], None, OP.is_le, None, cum)
+    h = scan(T.su2[:], T.rst2[:], T.cm2[:], h)
+    vcopy(T.nq[:, 0:2], T.su2[:, 255:512:256], h)
+    h = ts(T.nq[:, 2:4], T.acc2[:], 0.5, 128.0, OP.mult, OP.add, sa)
+    na = spread(4, lambda b, a: quad("na", b, slice(4 * a, 4 * a + 4)), lambda a: quad("nq", a, slice(0, 4)),
+                lambda b, a: T.na[64 * b:64 * b + 64, 8 * a:8 * a + 8], h)
+    oc = ts(T.offc[:], T.na[:], 255.0, None, OP.min, None, *na)
+    ck = pick("cc", L1, 256, 0, 256, T.offc[:], oc, a1, *own1)
+    own_c = vcopy(T.cl[:, 8 * me:8 * me + 1], size)
+    nwc = act(T.nwc[:], T.nw[:].indirect(T.offc[:]), oc, nw)
+
+    end = scan(T.end[:], T.one[:, 0:8], T.cl[:, 0:64:8], ("c2", nmsg), own_c)
+    h = ts(T.vi[:], T.rc[:], T.end[:, me - 1:me] if me else 0.0, None, OP.subtract, None, end)
+    h = ts(T.v7[:], T.vi[:], 7, None, OP.bitwise_and, None, h)
+    ts(T.off3[:, 0:20:2], T.v7[:], T.k8[:, 0:1], None, OP.add, None, h)
+    o3 = ts(T.off3[:, 1:20:2], T.v7[:], T.k8[:, 1:2], None, OP.add, None)
+    pc, ps = pick("slot3", CC, 256, 0, 128, T.off3[:, 0:8], o3, *ck)
+    send_cross("slot3c", "r3c", "rc3", pc)
+    send_cross("slot3s", "r3s", "rs3", ps)
+    n3 = act(T.n3[:], T.nwc[:].indirect(T.off3[:, 16:20]), o3, nwc)
+    pc, ps = pick("slot3", CC, 256, 128, 256, T.off3[:, 8:16], o3, *ck)
+    h = turn(T.nt3[:], T.n3[:], n3)
+    m3 = vcopy(T.m3[:], T.nt3[:, 0:64:32], h)
+    own_n3 = vcopy(T.nl3[:, 8 * me:8 * me + 1], T.nt3[:, 32:33])
+    note_out(T.m3, "rm3", "rn3", m3)
+    send_same("slot3c", "land3c", "a3", pc)
+    send_same("slot3s", "land3s", "a3", ps)
+    note_same(T.m3[:, 1:2], "nl3", "n3", m3)
+    i = pos.index(me)
+    own3 = pick("land3", CC, 256, 32 * me, 32 * me + 32, T.off3[:, 2 * i:2 * i + 2], o3, *ck)
+
+    h = ts(T.d256[:], T.cl[:, 0:64:8], -1.0, 256.0, OP.mult, OP.add)
+    for d in range(N):
+        h2 = ts(T.it[:, 1 + d:72:9], T.gg[:], T.end[:, d:d + 1], T.d256[:, d:d + 1], OP.is_ge, OP.mult, h)
+    h = scan(T.its[:], T.rst9[:], T.it[:], h2)
+    h = vcopy(T.xi[:], T.its[:, 8:72:9], h)
+    h = ts(T.xsh[:], T.xi[:], 3, None, OP.logical_shift_right, None, h)
+    oz = ts(T.offz[:], T.xsh[:], 256.0, None, OP.min, None, h)
+
+    a3 = ("a3", 2 * ncol)
+    fc = pickc(T.fq[:], T.land3c[:], T.offz[:], a3, ldz, oz, *own3)
+    fs = act(T.fs[:], T.land3s[:].indirect(T.offz[:]), a3, ldz, oz, *own3)
+    yp = do("t", lambda: E.matmul_mx(T.yp[:, 0:128], T.wq[:], T.ws[:], T.fq[:], T.fs[:], True, True), fc, fs, c_all)
+    load("y", "dout", T.oc[:], T.fq[:].bitcast(dt.uint8), fc)
+    h = vcopy(T.nf[:, 0:256:32], T.nl3[:, 0:64:8], ("n3", nmsg), own_n3)
+    h = turn(T.nft[:, 0:256], T.nf[:], h)
+    no = do("v", lambda: V.tensor_copy(T.no[:], T.nft[:].indirect(T.offz[:])), h)
+    for k in range(4):
+        load("y", "dout", T.osc[4 * k:4 * k + 4, :], T.fs[32 * k:32 * k + 4, :], fs)
+    ys = act(T.ysb[:], T.yp[:, 0:128], yp)
+    load("s", "dout", T.y[:], T.ysb[:], ys)
+    load("y", "dout", T.num[:], T.no[32 * am:32 * am + 1, :], no)
+    wait("p", [(s, cnt[s]) for s in ("qv", "qs", "qt", "qp", "dout", "ls", "ldz", "ldp", "ldx", "ldw")])

@@ -4,32 +4,28 @@ from concourse.mybir import dt, AluOpType, AxisListType, ActivationFunctionType
 OP = AluOpType
 COPY = ActivationFunctionType.Copy
 IDENT = ActivationFunctionType.Identity
-SIGN = ActivationFunctionType.Sign
 X = AxisListType.X
 N, P, L, CAPP = 8, 128, 3, 32
 BIG = 1.0e29
+AT = 6
 
 SCRATCH = {}
 for _kind, _list in {
-    "bfloat16": "plh 512 xh 520 wh 512 rstb 384 rst2 512 one 32 bits 384 bs 384 mt 256 cu 256 cm 256 junk1 256 "
-                "tt 64 cum 256 cm2 512 su2 512 junk3 512 cl 64 rm2 1 m1 2 nl1 64 rm1 1 n8 8",
-    "float8_e4m3fn_x4": "plc 128 prc 384 xq 130 wq 128 slot1c 256 land1c 256 ccc 256 slot3c 256 land3c 258 fq 128 r1c 64 r3c 64",
-    "uint8": "pls 128 prs 384 xs 130 ws 128 slot1s 256 land1s 256 ccs 256 slot3s 256 land3s 258 fs 128 r1s 64 r3s 64",
-    "uint16": "ofp 24 off1 16 offc 16 off3 20 nl3 64 m3 2 offz 8 rm3 1",
-    "int32": "pb 4 vi 10 v7 10 xi 8 xsh 8",
-    "float32": "rst9 72 pbf 4 nx 1 off 24 c32 64 ccr 256 c128 8 rhc 4 rh 4 bi 4 rq 4 bq 4 ggc 8 gg 8 k8 2 dm0 128 dm 128 cp 2 tri 384 "
-               "rc 10 dq 2 acc1 2 la1 2 em 8 ep 8 k0 1 ab 64 ab1 64 ab2 64 pd 256 junk2 256 thr 2 xg 384 nb 256 nt 256 "
-               "nw 256 acc2 2 nq 4 na 16 nwc 256 end 8 n3 64 nt3 64 d256 8 it 72 its 72 nf 256 nft 264 no 128 ysb 128",
+    "bfloat16": "xh 536 wh 512 dd 128 tm 256 m2 256 tx 32 t2x 32 r2 256 r1 256 t1 544 t2 576 t3 528 t4 576 c3 528 lb 16 m1 16 "
+                "one 8 cl 64 rm2 1 nl1 64 rm1 1 pbh 10 bt 4 bk 2 key 2 uvf 4 v16 16 sg 2 n8 8 ms 2",
+    "float8_e4m3fn_x4": "xq 134 wq 128 q1 136 q2 144 q3 132 q4 144 slot1c 256 land1c 256 slot3c 256 land3c 258 fq 128 r1c 64 r3c 64",
+    "uint8": "xs 134 ws 128 s1 136 s2 144 s3 132 s4 144 slot1s 256 land1s 256 slot3s 256 land3s 258 fs 128 r1s 64 r3s 64",
+    "uint16": "ofm 2 off1 16 ov 4 off3 16 offn 16 nl3 64 m3 2 offz 8 rm3 1",
+    "int32": "pb 8 ti 2 uv 4 vi 2 xi 8 xsh 8",
+    "float32": "i8 8 pt 8 rst9 72 c128 8 gg 8 k8 1 dm 128 tri 256 kv 64 kt 64 kk 2 kq 2 vx 2 pd 256 thr 2 xg 384 "
+               "nb 256 nt 256 nw 256 qd 2 plw 16 n3 64 nt3 64 end 8 d256 8 it 72 its 72 nf 256 nft 264 no 128 ysb 128 "
+               "em 8 ng 8 ee 8 e2 1 na 8 nk8 8 nk 8 junk 256 bias 8",
 }.items():
     _w = _list.split()
     for _i in range(0, len(_w), 2):
         SCRATCH[_w[_i]] = ("sbuf", [128, int(_w[_i + 1])], _kind)
-for _n in ("z0", "z1", "z2", "ga", "gb", "yp"):
+for _n in ("z", "cn", "lp", "ga", "gb", "sp", "pp", "yp"):
     SCRATCH[_n] = ("psum", [128, 512], "float32")
-SCRATCH["tw"] = ("sbuf", [128, 2, 32], "bfloat16")
-SCRATCH["bc"] = ("sbuf", [128, 2, 128], "bfloat16")
-SCRATCH["lq"] = ("sbuf", [128, 2, 2], "float32")
-SCRATCH["la"] = ("sbuf", [128, 2, 8], "float32")
 SEMAPHORES = ["qv", "qs", "qt", "qp", "ldp", "ldx", "ldw", "ldz", "dout", "ls",
               "a1", "n1", "c2", "a3", "n3", "rc1", "rs1", "rn1", "rn2", "rc3", "rs3", "rn3"]
 
@@ -80,9 +76,9 @@ def relay_program(g, core, T, topo, s, group):
         go(sem, [RemoteDMATransfer(dst_ids=[dest(topo, core, d) for d in to], dma_engine_mask=eng(topo, core, to[0], 0, 8), remote_sem=T.sem[rsem],
                                    srcs=[T[src][:]], dsts=[T[land][:, 8 * s:8 * s + 1]] * 2)])
 
-    note("rn1", "rm1", "nl1", "n1")
     cols("rc1", "r1c", "land1c", "a1")
     cols("rs1", "r1s", "land1s", "a1")
+    note("rn1", "rm1", "nl1", "n1")
     note("rn2", "rm2", "cl", "c2")
     cols("rc3", "r3c", "land3c", "a3")
     cols("rs3", "r3s", "land3s", "a3")
@@ -101,6 +97,8 @@ def rank_program(g, core, T, topo):
         return
     same, cross, relays = same_all[me], cross_all[me], relays_all[me]
     pos = cross + same
+    steps = [[pos[k] - pos[0], 2] for k in (4, 2, 1)]
+    assert pos == [pos[0] + sum(steps[b][0] * (i >> 2 - b & 1) for b in range(3)) for i in range(N)]
     am = same.index(me)
     peer = [r for r in same if r != me and T.cores[r] in topo.cores_of(core)]
     far = [r for r in same if r != me and r not in peer]
@@ -150,11 +148,8 @@ def rank_program(g, core, T, topo):
     def red(out, in_, op, *deps):
         return do("v", lambda: V.tensor_reduce(out, in_, X, op), *deps)
 
-    def scan(out, d0, d1, *deps, init=0.0, op1=OP.add):
-        return do("v", lambda: V.tensor_tensor_scan(out, d0, d1, init, OP.mult, op1), *deps)
-
-    def runs(out, in_, *deps):
-        return do("v", lambda: V.tensor_tensor_scan(out, in_, in_, 0.0, OP.add, OP.max), *deps)
+    def scan(out, d0, d1, *deps):
+        return do("v", lambda: V.tensor_tensor_scan(out, d0, d1, 0.0, OP.mult, OP.add), *deps)
 
     def turn(out, in_, *deps):
         return do("v", lambda: V.transpose(out, in_), *deps)
@@ -162,26 +157,23 @@ def rank_program(g, core, T, topo):
     def act(out, in_, *deps):
         return do("s", lambda: S.activation(out, in_, COPY), *deps)
 
-    def affine(out, in_, scale, bias, *deps):
-        return do("s", lambda: S.activation(out, in_, IDENT, bias, scale), *deps)
-
-    def count_s(out, junk, in_, bias, *deps):
-        return do("s", lambda: S.activation(junk, in_, SIGN, bias, -1.0, accum_out=out), *deps)
+    def lin(out, in_, scale, bias, *deps):
+        return do("s", lambda: S.activation(out, in_, COPY if isinstance(bias, float) else IDENT, bias, scale), *deps)
 
     def iota(ap, pattern, base, cm=0, flag=True):
-        last = ("qp", cnt.get("qp", 0))
         if flag:
-            return do("p", lambda: g.iota(ap, pattern, base, cm, allow_small_or_imprecise_dtypes=True), last)
-        return do("p", lambda: g.iota(ap, pattern, base, cm), last)
+            return do("p", lambda: g.iota(ap, pattern, base, cm, allow_small_or_imprecise_dtypes=True))
+        return do("p", lambda: g.iota(ap, pattern, base, cm))
 
-    def spread(ns, out, in_, half, *deps):
-        for k in range(8):
-            a, b = k // 2, k // 2 ^ k % 2
-            if k * ns % 8 < ns:
-                hs = act(out(b, a), in_(a), *deps)
-            else:
-                hv = vcopy(out(b, a), in_(a), *deps)
-        return vcopy(half(1, 0), half(0, 0), hv, hs), act(half(0, 1), half(1, 1), hv, hs)
+    def cast(out, in_, *deps):
+        return do("p", lambda: g.partition_broadcast(out, in_, 128), *deps)
+
+    def mm(out, n, q, s, a, b, *deps):
+        return do("t", lambda: E.matmul_mx(out[:, 0:n], q[:, a:a + 128], s[:, a:a + 128], q[:, b:b + n], s[:, b:b + n], True, True), *deps)
+
+    def count(k, tile, lead, out, *deps):
+        q, s = T["q" + k], T["s" + k]
+        return mm(out, 128, q, s, lead, 0, do("v", lambda: V.quantize_mx(q[:], s[:], tile[:]), *deps))
 
     def quad(t, a, *cols):
         return T[t][(slice(32 * a, 32 * a + 32),) + cols]
@@ -214,196 +206,219 @@ def rank_program(g, core, T, topo):
     def note(src, land, sem, to, ab):
         return xfer(src, T[land][:, 8 * me:8 * me + 1], [T.cores[r] for r in to], ab, sem)
 
-    def note_out(src, rbuf, rsem, *deps):
-        send([xfer(src[:, 0:1], T[rbuf][:], relays, MSG["relay"], rsem)], *deps)
+    def note_out(src, rbuf, sem, *deps):
+        send([xfer(src, T[rbuf][:], [k], HAND[i], sem) for i, k in enumerate(relays)], *deps)
 
     def note_same(src, land, sem, *deps):
         send([note(src, land, sem, far, MSG["far"]), note(src, land, sem, peer, MSG["peer"])], *deps)
 
-    ldp = load("y", "ldp", T.plh[:, 0:16], T.pl[:, 0:16])
-    ldx = load("s", "ldx", T.xh[:, 0:512], T.x[:])
+    ldp = load("y", "ldp", T.xh[:, 8:4 * AT], T.pl[:, 0:16])
+    ldx = load("s", "ldx", T.xh[:, 4 * AT:536], T.x[:])
     ldw = load("y", "ldw", T.wh[:], T.w[:], ldx)
-    i_of = iota(T.off[:], [[1, L], [0, 8]], 0)
-    i_p = iota(T.pb[:, 0:1], [[1, 1]], 0, 1, False)
-    i_rh = iota(T.rhc[:], [[16, 4]], 0)
-    for a in range(4):
-        i_dq = iota(quad("dq", a, slice(0, 2)), [[pos[4 + a] - pos[a], 2]], pos[a])
-    iota(T.c128[:], [[128, 8]], 0)
-    iota(T.ggc[:], [[128, 8]], me)
-    iota(T.cp[:], [[128, 2]], 0, 1)
-    iota(T.c32[:], [[128, 2], [0, 32]], 0, 1)
-    i_cc = iota(T.ccr[:], [[-1, 256]], 255)
-    c_pl = vset(T.plh[:, 16:512], 0.0)
-    h = vset(T.rstb[:], 1.0)
-    c_of = vcopy(T.ofp[:], T.off[:], i_of)
-    c_x = vset(T.xh[:, 512:520], 0.0)
-    ts(T.pb[:, 1:2], T.pb[:, 0:1], 15, None, OP.bitwise_and, None, i_p)
-    ts(T.pb[:, 2:3], T.pb[:, 0:1], 4, 1, OP.logical_shift_right, OP.bitwise_and)
-    h2 = ts(T.pb[:, 3:4], T.pb[:, 0:1], 5, None, OP.logical_shift_right, None)
-    c_rb = vset(T.rstb[:, 0:384:3], 0.0, h)
-    c_pb = vcopy(T.pbf[:], T.pb[:], h2)
-    rho, p16, p32 = [T.pbf[:, i:i + 1] for i in (1, 2, 3)]
-    c_rh = affine(T.rh[:], T.rhc[:], 1.0, rho, c_pb, i_rh)
-
-    plq = do("v", lambda: V.quantize_mx(T.plc[:], T.pls[:], T.plh[:]), ldp, c_pl)
-    pr = []
-    for b in range(L):
-        w, o = slice(128 * b, 128 * b + 128), slice(8 * b, 8 * b + 8)
-        hv = pickc(T.prc[:, w], T.plc[:], T.ofp[:, o], plq, c_of)
-        pr.append((hv, act(T.prs[:, w], T.pls[:].indirect(T.ofp[:, o]), plq, c_of)))
-        if b == 0:
-            xq = do("v", lambda: V.quantize_mx(T.xq[:], T.xs[:], T.xh[:]), ldx, c_x)
-    ts(T.nx[:], p16, -1.0, 1.0, OP.mult, OP.add, c_pb)
-    c_bi = ts(T.bi[:], T.rhc[:], rho, 0.5, OP.add, OP.add, i_rh)
-    zs = [T.z0, T.z1, T.z2]
-    for b in range(L):
-        w = slice(128 * b, 128 * b + 128)
-        z = do("t", lambda: E.matmul_mx(zs[b][:, 0:128], T.prc[:, w], T.prs[:, w], T.xq[:, 0:128], T.xs[:, 0:128], True, True), xq, *pr[b])
-        h = ts(T.bits[:, b:384:3], zs[b][:, 0:128], 0.0, float(2 ** b), OP.is_lt, OP.mult, z)
-    bs = scan(T.bs[:], T.rstb[:], T.bits[:], h, c_rb)
-
-    XQ, L1, CC = ("xq", "xs"), ("land1c", "land1s"), ("ccc", "ccs")
-    w2 = [slice(128 * e, 128 * e + 128) for e in range(2)]
-    hm = [ts(T.mt[:, w], T.bs[:, 2:384:3], T.dq[:, e:e + 1], None, OP.is_equal, None, bs, i_dq) for e, w in enumerate(w2)]
-    cu = [runs(T.cu[:, w], T.mt[:, w], hm[e]) for e, w in enumerate(w2)]
-    hs = [count_s(T.acc1[:, e:e + 1], T.junk1[:, w], T.cu[:, w], T.bi[:, 1:2], cu[e], c_bi) for e, w in enumerate(w2)]
-    hc = [ts(T.cm[:, w], T.cu[:, w], T.rh[:, 0:1], None, OP.is_le, None, cu[e], c_rh) for e, w in enumerate(w2)]
-    h0 = [red(T.lq[:, e, 0:1], T.cm[:, w], OP.add, hc[e]) for e, w in enumerate(w2)]
-    hl = ts(T.la1[:], T.lq[:, :, 0], T.nx[:, 0:1], None, OP.mult, None, *h0)
-    for e in range(2):
-        lq = ts(T.lq[:, e, 1:2], T.acc1[:, e:e + 1], 0.5, 64.0, OP.mult, OP.add, hs[e])
-        m1 = affine(T.m1[:, e:e + 1], T.lq[:, e, 1:2], p16, T.la1[:, e:e + 1], lq, hl)
-        if e == 0:
-            note_out(T.m1, "rm1", "rn1", m1)
-    la = spread(3, lambda b, a: quad("la", b, slice(0, 2), slice(2 * a, 2 * a + 2)), lambda a: quad("lq", a, slice(0, 2), slice(0, 2)),
-                lambda b, a: T.la[64 * b:64 * b + 64, :, 4 * a:4 * a + 4], lq, *h0)
-    o0 = vcopy(T.off1[:, 0:8], T.la[:, 0, :], *la)
-    o1 = vcopy(T.off1[:, 8:16], T.la[:, 1, :])
-    pc, ps = pick("slot1", XQ, 130, 0, 128, T.off1[:, 0:8], o0, xq)
-    send_cross("slot1c", "r1c", "rc1", pc)
-    send_cross("slot1s", "r1s", "rs1", ps)
-    note_same(T.m1[:, 1:2], "nl1", "n1", m1)
-    pc, ps = pick("slot1", XQ, 130, 128, 256, T.off1[:, 8:16], o1, xq)
-    send_same("slot1c", "land1c", "a1", pc)
-    send_same("slot1s", "land1s", "a1", ps)
-    i = pos.index(me)
-    own1 = pick("land1", XQ, 130, 32 * me, 32 * me + 32, T.off1[:, 2 * i:2 * i + 2], o1, xq)
-    own_n = vcopy(T.nl1[:, 8 * me:8 * me + 1], T.m1[:, 1:2], m1)
-
-    load("y", "ldz", T.land3c[:, 256:258].bitcast(dt.uint8), T.xq[:, 128:130].bitcast(dt.uint8), xq)
-    ldz = load("y", "ldz", T.land3s[:, 256:258], T.xs[:, 128:130], xq)
-    c_nb = vset(T.nb[:], 0.0)
-    h = vset(T.dm0[:], 0.9375)
-    c_dm = do("p", lambda: g.affine_select(T.dm[:], T.dm0[:], [[-1, 128]], OP.is_equal, 0.0, 0, 1), h, i_cc)
+    i_d = iota(T.dd[:], [[1, 128]], 0, -1)
+    i_8 = iota(T.i8[:], [[1, 8]], 0)
+    i_p = iota(T.pb[:, 0:2], [[-AT, 2]], AT, 1, False)
+    i_t = iota(T.pt[:], steps, pos[0])
+    i_r = iota(T.r2[:], [[0, 8], [1, 16], [16, 2]], 128)
+    i_1 = iota(T.r1[:], [[0, 8], [1, 16], [0, 2]], 0)
+    iota(T.v16[:], [[1, 8], [128, 2]], 0)
+    i_c = iota(T.c128[:], [[128, 8]], -AT)
+    c_x = vset(T.xh[:, 0:8], 0.0)
+    c_tx = vset(T.tx[:], 99.0)
+    c_t2 = vset(T.t2x[:], 99.0)
+    vset(T.t1[:, 34:544:4], 0.0)
+    c_c3 = vset(T.c3[:], 0.0)
+    ts(T.tm[:, 0:128], T.dd[:], 0.0, 127.0, OP.is_equal, OP.mult, i_d)
+    h = ts(T.tm[:, 128:256], T.dd[:], 0.0, None, OP.is_ge, None)
+    ts(T.pb[:, 2:4], T.pb[:, 0:2], 240, None, OP.bitwise_and, None, i_p)
+    ts(T.pb[:, 4:6], T.pb[:, 0:2], 15, None, OP.bitwise_and, None)
+    c_m = tt(T.t1[:, 32:544:4], T.tm[:, 0:128], T.tm[:, 128:256], OP.add, h)
+    ts(T.pb[:, 6:7], T.pb[:, 1:2], 4, None, OP.logical_shift_right, None)
+    h = ts(T.pb[:, 7:8], T.pb[:, 1:2], 1, None, OP.bitwise_and, None)
     for b in range(2):
-        w = 128 + 128 * b
-        c_tri = ts(T.tri[:, 128 * b:128 * b + w], T.ccr[:, 256 - w:256], T.cp[:, b:b + 1], BIG, OP.is_lt, OP.mult, i_cc)
-    c_one = vset(T.one[:], 1.0)
-    h = vset(T.rst2[:], 1.0)
-    c_r2 = vset(T.rst2[:, 0:512:256], 0.0, h)
-    h = vset(T.rst9[:], 1.0)
-    vset(T.rst9[:, 0:72:9], 0.0, h)
-    h = ts(T.k8[:, 0:1], p32, 64.0, rho, OP.mult, OP.add)
-    h = ts(T.rq[:], T.rhc[:], T.k8[:, 0:1], None, OP.add, None, h)
-    c_bq = ts(T.bq[:], T.rq[:], 0.5, None, OP.add, None, h)
-    h = ts(T.k8[:, 0:1], rho, 8.0, None, OP.mult, None, c_bq)
-    ts(T.k8[:, 1:2], T.k8[:, 0:1], 128.0, None, OP.add, None, h)
-    c_gg = ts(T.gg[:], T.ggc[:], T.k8[:, 0:1], None, OP.add, None, h)
-    vcopy(T.it[:, 0:72:9], T.gg[:], c_gg)
-    for i in range(N):
-        vset(T.rc[:, i:i + 1], 2048.0 + pos[i])
-    ts(T.rc[:, 8:10], T.dq[:], 2048.0, None, OP.add, None)
-    vset(T.nf[:], 0.0)
-    vset(T.nft[:, 256:264], -1.0)
-    c_all = do("v", lambda: V.quantize_mx(T.wq[:], T.ws[:], T.wh[:]), ldw)
+        h2 = vset(T.c3[:, 264 * b:264 * b + 8], BIG, c_c3)
+    c_pb = vcopy(T.pbh[:, 0:8], T.pb[:], h)
+    for k in (0, 3, 5):
+        c_tx2 = act(T.tx[:, k:32:8], T.i8[:, 0:4], i_8, c_tx)
+    act(T.m2[:, 0:256:2], T.t1[:, 32:544:4], c_m)
+    c_m2 = lin(T.m2[:, 1:256:2], T.t1[:, 32:544:4], -1.0, 0.0)
+    for k in (0, 3):
+        c_t22 = act(T.t2x[:, k:32:4], T.pt[:], i_t, c_t2)
+    for k in (1, 2, 5, 265, 268):
+        c_s3 = lin(T.c3[:, k:k + 1], T.i8[:, 0:1], 0.0, 0.0, h2)
+    col = [T.pbh[:, i:i + 1] for i in range(10)]
+    rho, odd = col[5], col[7]
+
+    xq = do("v", lambda: V.quantize_mx(T.xq[:], T.xs[:], T.xh[:]), ldx, ldp, c_x)
+    z = mm(T.z, 128, T.xq, T.xs, AT, 0, xq)
+    c_om = ts(T.ofm[:, 0:1], odd, 8.0, col[6], OP.mult, OP.add, c_pb)
+    for b in range(2):
+        c_c3 = ts(T.c3[:, 264 * b + 8:264 * b + 264:2], T.dd[:], 0.0, BIG, OP.is_lt, OP.mult)
+    b0, b1, b2 = [T.bt[:, i:i + 1] for i in range(3)]
+    h0 = ts(T.bt[:, 0:2], T.z[:, 2:4], 0.0, None, OP.is_lt, None, z)
+    h1 = ts(b2, T.z[:, 4:5], 0.0, 2.0, OP.is_lt, OP.mult)
+    ts(T.t1[:, 33:544:2], T.m2[:], b0, None, OP.mult, None, h0, c_m2)
+    h = ts(T.t1[:, 0:32], T.tx[:], b1, b2, OP.subtract, OP.is_equal, h1, c_tx2)
+    hb = ts(T.bk[:, 0:1], b1, b2, 2.0, OP.add, OP.mult)
+    cn = count("1", T.t1, 8, T.cn, h)
+    h = ts(T.bk[:, 1:2], T.bk[:, 0:1], b0, None, OP.add, None, hb)
+    for k in range(2):
+        ts(T.t2[:, k:64:2], T.t2x[:], T.bk[:, 1:2], col[2 + 2 * k], OP.is_equal, OP.mult, h, c_t22)
+    h = red(T.key[:, 0:1], T.cn[:, 0:8], OP.max, cn)
+    for k in range(2):
+        h2 = ts(T.t2[:, 64 + k:576:2], T.r2[:], T.key[:, 0:1], None, OP.is_equal, None, h, i_r)
+    lp = count("2", T.t2, 16, T.lp, h2)
+    c_dm = ts(T.dm[:], T.dd[:], 0.0, 0.9375, OP.is_equal, OP.mult)
+    ts(T.tri[:, 0:128], T.dd[:, 127::-1], 0.0, BIG, OP.is_lt, OP.mult)
+    XQ, L1 = ("xq", "xs"), ("land1c", "land1s")
+    o1 = vcopy(T.off1[:], T.lp[:, 0:16], lp)
+    lb = vcopy(T.lb[:], T.lp[:, 0:16])
+    pk = [pick("slot1", XQ, 134, 128 * e, 128 * e + 128, T.off1[:, 8 * e:8 * e + 8], o1) for e in range(2)]
+    send_cross("slot1c", "r1c", "rc1", pk[0][0])
+    send_cross("slot1s", "r1s", "rs1", pk[0][1])
+    send_same("slot1c", "land1c", "a1", pk[1][0])
+    send_same("slot1s", "land1s", "a1", pk[1][1])
+    i = pos.index(me)
+    own1 = pick("land1", XQ, 134, 32 * me, 32 * me + 32, T.off1[:, 2 * i:2 * i + 2], o1)
+
+    e0, p0 = pos.index(0) // 4, 32 * (pos.index(0) % 4)
+    zz = mm(T.z, 128, T.slot1c, T.slot1s, 128 * e0, 128 * e0, h1, *pk[e0])
+    m1 = act(T.m1[:], T.lb[:].indirect(T.ofm[:, 0:1]), lb, c_om)
+    h = ts(T.sg[p0:p0 + 1, 0:1], T.z[p0:p0 + 1, p0:p0 + 1], 0.0, 2.0, OP.is_gt, OP.mult, zz)
+    h2 = vcopy(T.ms[:], T.m1[:, 0:2], m1)
+    m1 = ts(T.ms[p0:p0 + 1, e0:e0 + 1], T.sg[p0:p0 + 1, 0:1], -1.0, T.m1[p0:p0 + 1, e0:e0 + 1], OP.add, OP.mult, h, h2)
+    note_out(T.ms[:, 0:1], "rm1", "rn1", m1)
+    note_same(T.ms[:, 1:2], "nl1", "n1")
+
+    load("y", "ldz", T.land3c[:, 256:258].bitcast(dt.uint8), T.xq[:, 0:2].bitcast(dt.uint8), xq)
+    ldz = load("y", "ldz", T.land3s[:, 256:258], T.xs[:, 0:2], xq)
+    c_tri = vset(T.tri[:, 128:256], BIG)
+    own_n = vcopy(T.nl1[:, 8 * me:8 * me + 1], T.ms[:, 1:2], m1)
+    lin(T.nb[:], T.r2[:], 0.0, 0.0, i_r)
+    lin(T.nf[:], T.r2[:], 0.0, 0.0)
+    for k in range(2):
+        for j in range(2):
+            h = lin(T.kv[:, 16 * j + k:16 * j + 16:2], T.pt[:], 2.0, 4096.0 + k)
+    for a in range(4):
+        for k in range(4):
+            h2 = vset(quad("kv", a, slice(32 + k, 64, 4)), 4096.0 + 2 * pos[4 * (k // 2) + a] + k % 2)
+    lin(T.one[:], T.i8[:], 0.0, 1.0)
+    h3 = lin(T.rst9[:], T.r2[:, 0:72], 0.0, 1.0)
+    lin(col[8], col[3], 1.0, 128.0, c_pb)
+    h4 = lin(T.k8[:], rho, 16.0, 2.0 * me)
+    lin(T.nft[:, 256:264], T.i8[:], 0.0, -1.0)
+    lin(T.rst9[:, 0:72:9], T.i8[:], 0.0, 0.0, h3)
+    lin(T.gg[:], T.i8[:], 256.0, T.k8[:, 0:1], h4)
+    c_s = lin(T.it[:, 0:72:9], T.i8[:], 256.0, T.k8[:, 0:1])
+    c_w = do("v", lambda: V.quantize_mx(T.wq[:], T.ws[:], T.wh[:]), ldw)
+    h = turn(T.kt[:], T.kv[:], h, h2)
+    vcopy(T.kk[:], T.kt[:, 0:64:32], h)
+    c_k = ts(T.kq[:], T.kt[:, 0:64:32], -7.5, None, OP.add, None)
 
     a1, n1 = ("a1", 2 * ncol), ("n1", nmsg)
-    h = tt(T.nb[:, 0:256:32], T.nl1[:, 0:64:8], T.c128[:], OP.add, n1, own_n, c_nb, i_cc)
-    nt = turn(T.nt[:], T.nb[:], h)
-    n8 = do("p", lambda: g.partition_broadcast(T.n8[:], T.nl1[32 * am:32 * am + 1, 0:64:8], 128), n1, own_n, c_dm)
-    nw = do("p", lambda: g.partition_broadcast(T.nw[:], T.nt[32 * am:32 * am + 1, :], 128), nt, n8)
-    h = ts(T.em[:], T.n8[:], P - 1.0, None, OP.is_gt, None, n8)
-    h = scan(T.ep[:], T.em[:], T.one[:, 0:8], h, c_one, init=32.0, op1=OP.mult)
-    h = red(T.k0[:], T.ep[:], OP.add, h)
-    ts(T.ab1[:], T.c32[:], T.k0[:, 0:1], -2 * BIG, OP.is_equal, OP.mult, h)
-    h = ts(T.ab2[:], T.c32[:], T.k0[:, 0:1], 2 * BIG, OP.is_lt, OP.mult)
-    ab = tt(T.ab[:], T.ab1[:], T.ab2[:], OP.add, h)
-
-    gs, gm = [T.ga, T.gb], []
+    gs = [T.ga, T.gb]
     wd = [(slice(128 * b, 128 * b + 128), slice(128 * b, 128 + 256 * b), 128 + 128 * b) for b in range(2)]
-    for b in range(2):
-        w, w2, n = wd[b]
-        gm.append(do("t", lambda: E.matmul_mx(gs[b][:, 0:n], T.land1c[:, w], T.land1s[:, w], T.land1c[:, 0:n], T.land1s[:, 0:n], True, True), a1, *own1))
-    mx, th, hl, tr = [], [], [], []
+    gm = [mm(gs[b], wd[b][2], T.land1c, T.land1s, 128 * b, 0, a1, *own1) for b in range(2)]
+    if me == 0:
+        n8 = cast(T.n8[:], T.nl1[32 * am:32 * am + 1, 0:64:8], n1, own_n)
+    mx, th = [], []
     for b in range(2):
         w, w2, n = wd[b]
         h = tt(T.pd[:, w], gs[b][:, w], T.dm[:], OP.mult, gm[b], c_dm)
-        th.append(do("s", lambda: S.activation(T.junk2[:, w], T.pd[:, w], COPY, accum_out=T.thr[:, b:b + 1]), h))
-        mx.append(do("v", lambda: V.tensor_tensor_scan(T.xg[:, w2], gs[b][:, n - 1::-1], T.tri[:, w2], 0.0, OP.max, OP.min), c_tri))
+        th.append(do("s", lambda: S.activation(T.junk[:, w], T.pd[:, w], COPY, accum_out=T.thr[:, b:b + 1]), h))
+        mx.append(do("v", lambda: V.tensor_tensor_scan(T.xg[:, w2], gs[b][:, n - 1::-1], T.tri[:, 0:n], 0.0, OP.max, OP.min), c_tri))
     for b in range(2):
-        w = slice(32 * b, 32 * b + 32)
         at = 128 * b + wd[b][2] - 1
-        hl.append(ts(T.tt[:, w], T.ab[:, w], T.xg[:, at:at + 1], T.thr[:, b:b + 1], OP.add, OP.is_lt, mx[b], th[b], ab))
-    for b in range(2):
-        tr.append(turn(T.tw[:, b, :], T.tt[:, 32 * b:32 * b + 32], hl[b]))
-    bc = spread(4, lambda b, a: quad("bc", b, slice(0, 2), slice(32 * a, 32 * a + 32)), lambda a: quad("tw", a, slice(0, 2), slice(0, 32)),
-                lambda b, a: T.bc[64 * b:64 * b + 64, :, 64 * a:64 * a + 64], *tr)
-    h = scan(T.cum[:, 0:128], T.rst2[:, 1:129], T.bc[:, 0, :], *bc)
-    cum = scan(T.cum[:, 128:256], T.rst2[:, 1:129], T.bc[:, 1, :], h, c_r2, init=T.cum[:, 127:128])
+        t3 = ts(T.t3[:, b:528:2], T.c3[:, 264 * b:264 * b + 264], T.xg[:, at:at + 1], T.thr[:, b:b + 1], OP.add, OP.is_lt, mx[b], th[b], c_c3, c_s3)
+    if me == 0:
+        ts(T.em[:], T.n8[:], 0.0, None, OP.is_equal, None, n8)
+        h = ts(T.ng[:], T.n8[:], 0.0, None, OP.is_lt, None)
+    sp = count("3", T.t3, 4, T.sp, t3)
+    size = T.cl[:, 8 * me:8 * me + 1]
+    qd = ts(T.qd[:], T.t3[:, 2:4], -257.0, 256.0, OP.mult, OP.add)
+    if me == 0:
+        he = scan(T.ee[:], T.em[:, 7::-1], T.ng[:, 7::-1], h)
+        hn = lin(T.na[:], T.nl1[:, 0:64:8], 1.0, 0.0, n1, own_n)
+        hn = do("s", lambda: S.activation(T.na[:], T.na[:], ActivationFunctionType.Abs), hn)
+        nb = tt(T.nb[:, 0:256:32], T.na[:], T.c128[:], OP.add, hn, c_s, i_c)
+        sz = ts(size, T.sp[:, 0:1], T.ee[:, 7:8], 2.0, OP.add, OP.mult, sp, he)
+    else:
+        nb = tt(T.nb[:, 0:256:32], T.nl1[:, 0:64:8], T.c128[:], OP.add, n1, own_n, c_s, i_c)
+        sz = ts(size, T.sp[:, 0:1], 2.0, None, OP.mult, None, sp)
 
-    size = T.cum[:, 255:256]
-    send([xfer(size, T.rm2[:], [k], HAND[i], "rn2") for i, k in enumerate(relays)], cum)
+    note_out(size, "rm2", "rn2", sz)
     note_same(size, "cl", "c2")
-    for c in range(2):
-        w = slice(256 * c, 256 * c + 256)
-        sa = count_s(T.acc2[:, c:c + 1], T.junk3[:, w], T.cum[:], T.bq[:, 2 + c:3 + c], cum, c_bq)
-        h = ts(T.cm2[:, w], T.cum[:], T.rq[:, c:c + 1], None, OP.is_le, None, cum)
-    h = scan(T.su2[:], T.rst2[:], T.cm2[:], h)
-    vcopy(T.nq[:, 0:2], T.su2[:, 255:512:256], h)
-    h = ts(T.nq[:, 2:4], T.acc2[:], 0.5, 128.0, OP.mult, OP.add, sa)
-    na = spread(4, lambda b, a: quad("na", b, slice(4 * a, 4 * a + 4)), lambda a: quad("nq", a, slice(0, 4)),
-                lambda b, a: T.na[64 * b:64 * b + 64, 8 * a:8 * a + 8], h)
-    oc = ts(T.offc[:], T.na[:], 255.0, None, OP.min, None, *na)
-    ck = pick("cc", L1, 256, 0, 256, T.offc[:], oc, a1, *own1)
-    own_c = vcopy(T.cl[:, 8 * me:8 * me + 1], size)
-    nwc = act(T.nwc[:], T.nw[:].indirect(T.offc[:]), oc, nw)
+    h = tt(T.ti[:], T.sp[:, 1:3], T.qd[:], OP.add, qd)
+    nt = turn(T.nt[:], T.nb[:], nb)
+    nw = cast(T.nw[:], T.nt[32 * am:32 * am + 1, :], nt)
+    ts(T.uv[:, 0:2], T.ti[:], 3, 15, OP.logical_shift_right, OP.bitwise_and, h)
+    h = ts(T.uv[:, 2:4], T.ti[:], 256 + 128 + 7, None, OP.bitwise_and, None)
+    if me == 0:
+        he = ts(T.e2[:], T.ee[:, 7:8], 2.0, None, OP.mult, None)
+    h = vcopy(T.uvf[:], T.uv[:], h)
+    for b in range(2):
+        for k in range(2):
+            ts(T.t4[:, b + 2 * k:64:4], T.v16[:], T.uvf[:, 2 + b:3 + b], rho if k else col[8 if b else 3], OP.is_equal, OP.mult, h)
+    for b in range(2):
+        h2 = ts(T.t4[:, 64 + b:576:2], T.r1[:], T.uvf[:, b:b + 1], None, OP.is_equal, None)
+    pp = count("4", T.t4, 16, T.pp, h2)
+    plw = act(T.plw[:], T.pp[:, 0:16], pp)
 
-    end = scan(T.end[:], T.one[:, 0:8], T.cl[:, 0:64:8], ("c2", nmsg), own_c)
-    h = ts(T.vi[:], T.rc[:], T.end[:, me - 1:me] if me else 0.0, None, OP.subtract, None, end)
-    h = ts(T.v7[:], T.vi[:], 7, None, OP.bitwise_and, None, h)
-    ts(T.off3[:, 0:20:2], T.v7[:], T.k8[:, 0:1], None, OP.add, None, h)
-    o3 = ts(T.off3[:, 1:20:2], T.v7[:], T.k8[:, 1:2], None, OP.add, None)
-    pc, ps = pick("slot3", CC, 256, 0, 128, T.off3[:, 0:8], o3, *ck)
+    c2 = ("c2", nmsg)
+    if me:
+        he = end = scan(T.end[:], T.one[:], T.cl[:, 0:64:8], c2, sz)
+    before = T.end[:, me - 1:me] if me else T.e2[:, 0:1]
+    ts(T.vi[:], T.kq[:], before, 0.0625, OP.subtract, OP.mult, he, c_k)
+    h = ts(T.vx[:], T.kk[:], before, None, OP.subtract, None)
+    if me:
+        hd = ts(T.d256[:], T.cl[:, 0:64:8], -1.0, 512.0, OP.mult, OP.add)
+    ov = [ts(T.ov[:, 2 * k:2 * k + 1], T.vi[:, k:k + 1], -16.0, T.vx[:, k:k + 1], OP.mult, OP.add, h) for k in range(2)]
+    o3 = vcopy(T.off3[:], T.plw[:].indirect(T.ov[:, 0:1]), ov[0], plw)
+    on = vcopy(T.offn[:], T.plw[:].indirect(T.ov[:, 2:3]), ov[1])
+    pc, ps = pick("slot3", L1, 256, 0, 128, T.off3[:, 0:8], o3, a1, *own1)
     send_cross("slot3c", "r3c", "rc3", pc)
     send_cross("slot3s", "r3s", "rs3", ps)
-    n3 = act(T.n3[:], T.nwc[:].indirect(T.off3[:, 16:20]), o3, nwc)
-    pc, ps = pick("slot3", CC, 256, 128, 256, T.off3[:, 8:16], o3, *ck)
+    n3 = act(T.n3[:], T.nw[:].indirect(T.offn[:, 0:4]), on, nw)
+    pc, ps = pick("slot3", L1, 256, 128, 256, T.off3[:, 8:16], o3)
     h = turn(T.nt3[:], T.n3[:], n3)
+    hc = pickc(T.land3c[:, 32 * me:32 * me + 32], T.land1c[:], T.off3[:, 2 * i:2 * i + 2])
     m3 = vcopy(T.m3[:], T.nt3[:, 0:64:32], h)
-    own_n3 = vcopy(T.nl3[:, 8 * me:8 * me + 1], T.nt3[:, 32:33])
-    note_out(T.m3, "rm3", "rn3", m3)
+    own3 = (hc, act(T.land3s[:, 32 * me:32 * me + 32], T.land1s[:].indirect(T.off3[:, 2 * i:2 * i + 2])))
     send_same("slot3c", "land3c", "a3", pc)
+    note_out(T.m3[:, 0:1], "rm3", "rn3", m3)
     send_same("slot3s", "land3s", "a3", ps)
-    note_same(T.m3[:, 1:2], "nl3", "n3", m3)
-    i = pos.index(me)
-    own3 = pick("land3", CC, 256, 32 * me, 32 * me + 32, T.off3[:, 2 * i:2 * i + 2], o3, *ck)
+    note_same(T.m3[:, 1:2], "nl3", "n3")
+    own_n3 = vcopy(T.nl3[:, 8 * me:8 * me + 1], T.nt3[:, 32:33])
 
-    h = ts(T.d256[:], T.cl[:, 0:64:8], -1.0, 256.0, OP.mult, OP.add)
+    if me == 0:
+        h = ts(T.nk8[:], T.n8[:], 0.0, -1.0, OP.min, OP.mult)
+        ts(T.it[:, 0:72:9], T.gg[:], T.e2[:, 0:1], None, OP.subtract, None)
+        h = tt(T.nk[:], T.nk8[:], T.c128[:], OP.add, h)
+        end = scan(T.end[:], T.one[:], T.cl[:, 0:64:8], c2)
+        h = ts(T.nk8[:], T.nk[:], 1.0, None, OP.add, None, h)
+        hd = ts(T.d256[:], T.cl[:, 0:64:8], -1.0, 512.0, OP.mult, OP.add)
+        h = tt(T.nk[:], T.nk8[:], T.ng[:], OP.mult, h)
+        hd = ts(T.d256[:, 0:1], T.d256[:, 0:1], T.e2[:, 0:1], None, OP.add, None, hd)
+        nk = scan(T.nk8[:], T.em[:, 7::-1], T.nk[:, 7::-1], h)
     for d in range(N):
-        h2 = ts(T.it[:, 1 + d:72:9], T.gg[:], T.end[:, d:d + 1], T.d256[:, d:d + 1], OP.is_ge, OP.mult, h)
+        h2 = ts(T.it[:, 1 + d:72:9], T.gg[:], T.end[:, d:d + 1], T.d256[:, d:d + 1], OP.is_ge, OP.mult, hd, end)
     h = scan(T.its[:], T.rst9[:], T.it[:], h2)
+    if me == 0:
+        nk = ts(T.nk[:, 0:1], T.nk8[:, 7:8], -1.0, None, OP.add, None, nk)
     h = vcopy(T.xi[:], T.its[:, 8:72:9], h)
-    h = ts(T.xsh[:], T.xi[:], 3, None, OP.logical_shift_right, None, h)
+    h = ts(T.xsh[:], T.xi[:], 4, None, OP.logical_shift_right, None, h)
     oz = ts(T.offz[:], T.xsh[:], 256.0, None, OP.min, None, h)
 
     a3 = ("a3", 2 * ncol)
     fc = pickc(T.fq[:], T.land3c[:], T.offz[:], a3, ldz, oz, *own3)
     fs = act(T.fs[:], T.land3s[:].indirect(T.offz[:]), a3, ldz, oz, *own3)
-    yp = do("t", lambda: E.matmul_mx(T.yp[:, 0:128], T.wq[:], T.ws[:], T.fq[:], T.fs[:], True, True), fc, fs, c_all)
+    yp = do("t", lambda: E.matmul_mx(T.yp[:, 0:128], T.wq[:], T.ws[:], T.fq[:], T.fs[:], True, True), fc, fs, c_w)
     load("y", "dout", T.oc[:], T.fq[:].bitcast(dt.uint8), fc)
     h = vcopy(T.nf[:, 0:256:32], T.nl3[:, 0:64:8], ("n3", nmsg), own_n3)
     h = turn(T.nft[:, 0:256], T.nf[:], h)
-    no = do("v", lambda: V.tensor_copy(T.no[:], T.nft[:].indirect(T.offz[:])), h)
+    no = vcopy(T.no[:], T.nft[:].indirect(T.offz[:]), h)
+    if me == 0:
+        no = ts(T.no[:, 0:1], T.no[:, 0:1], T.nk[:, 0:1], None, OP.max, None, no, nk)
     for k in range(4):
         load("y", "dout", T.osc[4 * k:4 * k + 4, :], T.fs[32 * k:32 * k + 4, :], fs)
     ys = act(T.ysb[:], T.yp[:, 0:128], yp)

@@ -2,8 +2,8 @@ from concourse.bass import DstId, RemoteDMATransfer
 from concourse.mybir import dt, AluOpType, AxisListType, ActivationFunctionType
 
 OP = AluOpType
-COPY = ActivationFunctionType.Copy
-IDENT = ActivationFunctionType.Identity
+FN = ActivationFunctionType
+COPY = FN.Copy
 X = AxisListType.X
 N, P, L, CAPP = 8, 128, 3, 32
 BIG = 1.0e29
@@ -11,15 +11,15 @@ AT = 6
 
 SCRATCH = {}
 for _kind, _list in {
-    "bfloat16": "xh 536 wh 512 dd 128 tm 256 m2 256 tx 32 t2x 32 r2 256 r1 256 t1 544 t2 576 t3 528 t4 576 c3 528 lb 16 m1 16 "
-                "one 8 cl 64 rm2 1 nl1 64 rm1 1 pbh 10 bt 4 bk 2 key 2 uvf 4 v16 16 sg 2 n8 8 ms 2",
-    "float8_e4m3fn_x4": "xq 134 wq 128 q1 136 q2 144 q3 132 q4 144 slot1c 256 land1c 256 slot3c 256 land3c 258 fq 128 r1c 64 r3c 64",
-    "uint8": "xs 134 ws 128 s1 136 s2 144 s3 132 s4 144 slot1s 256 land1s 256 slot3s 256 land3s 258 fs 128 r1s 64 r3s 64",
-    "uint16": "ofm 2 off1 16 ov 4 off3 16 offn 16 nl3 64 m3 2 offz 8 rm3 1",
+    "bfloat16": "xh 536 wh 512 dd 128 tm 256 m2 256 tx 32 t2x 32 r2 256 r1 128 t1 544 t2 576 t3 512 t5 528 t4 576 c3 656 "
+                "one 8 cl 64 rm2 1 pbh 10 bt 4 bk 2 key 2 uvf 4 v16 32 vv 2",
+    "float8_e4m3fn_x4": "xq 134 wq 128 q1 136 q2 144 q3 128 q5 132 q4 144 slot1c 256 land1c 256 slot3c 256 land3c 258 fq 128 r1c 64 r3c 64",
+    "uint8": "xs 134 ws 128 s1 136 s2 144 s3 128 s5 132 s4 144 slot1s 256 land1s 256 slot3s 256 land3s 258 fs 128 r1s 64 r3s 64",
+    "uint16": "rep 16 ms 2 nl1 64 rm1 1 off1 16 ov 4 off3 16 offn 16 nl3 64 m3 2 offz 8 rm3 1",
     "int32": "pb 8 ti 2 uv 4 vi 2 xi 8 xsh 8",
-    "float32": "i8 8 pt 8 rst9 72 c128 8 gg 8 k8 1 dm 128 tri 256 kv 64 kt 64 kk 2 kq 2 vx 2 pd 256 thr 2 xg 384 "
-               "nb 256 nt 256 nw 256 qd 2 plw 16 n3 64 nt3 64 end 8 d256 8 it 72 its 72 nf 256 nft 264 no 128 ysb 128 "
-               "em 8 ng 8 ee 8 e2 1 na 8 nk8 8 nk 8 junk 256 bias 8",
+    "float32": "i8 8 pt 8 rst9 72 c128 8 gg 8 k8 1 dm 128 tri 256 kv 64 kt 64 kk 4 vx 2 pd 256 thr 2 xg 384 "
+               "nb 256 nw 256 qd 2 plw 16 n3 64 nt3 64 end 8 d256 8 it 72 its 72 nf 256 nft 264 no 128 ysb 128 "
+               "en 24 e2 1 nk 24 junk 256 pf 4 sg 4 nlf 8 rp 256 rt 256 ab 256 rb 256 sm 256 mq 32 mr 32 wa 64 wb 64 wc 64 rf 16",
 }.items():
     _w = _list.split()
     for _i in range(0, len(_w), 2):
@@ -36,7 +36,9 @@ def wiring(T, topo):
     cross = [[r for r in range(N) if r not in same[s]] for s in range(N)]
     relays = [[k for k in topo.cores_of(c) if k not in cores and topo.die(k) == topo.die(c)
                and all(topo.may_write(k, cores[r]) for r in cross[s])][:2] for s, c in enumerate(cores)]
-    return same, cross, relays
+    pair = [[r for r in range(N) if cores[r] in topo.cores_of(c)] for c in cores]
+    assert all(len(p) == 2 and p[1] == p[0] + 1 for p in pair)
+    return same, cross, relays, pair
 
 
 def eng(topo, src, dst, a, b):
@@ -58,7 +60,7 @@ def view(T, buf, a, b):
     return v.bitcast(dt.uint8) if buf[-1] == "c" else v
 
 
-def relay_program(g, core, T, topo, s, group):
+def relay_program(g, core, T, topo, s, group, first, one):
     to = [T.cores[r] for r in group]
     sent = [0]
 
@@ -67,41 +69,42 @@ def relay_program(g, core, T, topo, s, group):
         g.remote_dma_fused(tr, local_sem=T.sem.ls)
         sent[0] += 8
 
-    def cols(sem, buf, land, rsem):
-        at = 32 * s
-        go(sem, [RemoteDMATransfer(dst_ids=[dest(topo, core, d)], dma_engine_mask=eng(topo, core, d, 4 * i, 4 * i + 4), remote_sem=T.sem[rsem],
-                                   src=view(T, buf, 32 * i, 32 * i + 32), dst=view(T, land, at, at + 32)) for i, d in enumerate(to)])
+    def write(d, a, b, rsem, src, dst):
+        return RemoteDMATransfer(dst_ids=[dest(topo, core, d)], dma_engine_mask=eng(topo, core, d, a, b), remote_sem=T.sem[rsem], src=src, dst=dst)
+
+    def cols(k):
+        go("rc" + k, [write(d, 4 * i, 4 * i + 4, "a" + k, view(T, "r%sc" % k, 32 * i, 32 * i + 32), view(T, "land%sc" % k, 32 * s, 32 * s + 32))
+                      for i, d in enumerate(to)])
+        go("rs" + k, [write(T.cores[one], 0, 8, "a" + k, T["r%ss" % k][:], T["land%ss" % k][:, 32 * first:32 * first + 64])])
 
     def note(sem, src, land, rsem):
         go(sem, [RemoteDMATransfer(dst_ids=[dest(topo, core, d) for d in to], dma_engine_mask=eng(topo, core, to[0], 0, 8), remote_sem=T.sem[rsem],
                                    srcs=[T[src][:]], dsts=[T[land][:, 8 * s:8 * s + 1]] * 2)])
 
-    cols("rc1", "r1c", "land1c", "a1")
-    cols("rs1", "r1s", "land1s", "a1")
     note("rn1", "rm1", "nl1", "n1")
+    cols("1")
     note("rn2", "rm2", "cl", "c2")
-    cols("rc3", "r3c", "land3c", "a3")
-    cols("rs3", "r3s", "land3s", "a3")
+    cols("3")
     note("rn3", "rm3", "nl3", "n3")
     g.wait_ge(T.sem.ls, sent[0])
 
 
 def rank_program(g, core, T, topo):
-    same_all, cross_all, relays_all = wiring(T, topo)
+    same_all, cross_all, relays_all, pair_all = wiring(T, topo)
     me = T.rank_of(core)
     if me is None:
         for s in range(N):
             if core in relays_all[s]:
                 i = relays_all[s].index(core)
-                relay_program(g, core, T, topo, s, cross_all[s][2 * i:2 * i + 2])
+                relay_program(g, core, T, topo, s, cross_all[s][2 * i:2 * i + 2], pair_all[s][0], cross_all[s][2 * i + pair_all[s].index(s)])
         return
-    same, cross, relays = same_all[me], cross_all[me], relays_all[me]
+    same, cross, relays, pair = same_all[me], cross_all[me], relays_all[me], pair_all[me]
     pos = cross + same
     steps = [[pos[k] - pos[0], 2] for k in (4, 2, 1)]
     assert pos == [pos[0] + sum(steps[b][0] * (i >> 2 - b & 1) for b in range(3)) for i in range(N)]
     am = same.index(me)
-    peer = [r for r in same if r != me and T.cores[r] in topo.cores_of(core)]
-    far = [r for r in same if r != me and r not in peer]
+    peer = [r for r in pair if r != me]
+    far = [r for r in same if r not in pair]
     ncol = 8 * len(peer) + 4 * len(far) + 4 * len(cross)
     nmsg = 8 * (N - 1)
 
@@ -148,8 +151,8 @@ def rank_program(g, core, T, topo):
     def red(out, in_, op, *deps):
         return do("v", lambda: V.tensor_reduce(out, in_, X, op), *deps)
 
-    def scan(out, d0, d1, *deps):
-        return do("v", lambda: V.tensor_tensor_scan(out, d0, d1, 0.0, OP.mult, OP.add), *deps)
+    def scan(out, d0, d1, *deps, ops=(OP.mult, OP.add)):
+        return do("v", lambda: V.tensor_tensor_scan(out, d0, d1, 0.0, *ops), *deps)
 
     def turn(out, in_, *deps):
         return do("v", lambda: V.transpose(out, in_), *deps)
@@ -157,8 +160,12 @@ def rank_program(g, core, T, topo):
     def act(out, in_, *deps):
         return do("s", lambda: S.activation(out, in_, COPY), *deps)
 
-    def lin(out, in_, scale, bias, *deps):
-        return do("s", lambda: S.activation(out, in_, COPY if isinstance(bias, float) else IDENT, bias, scale), *deps)
+    def lin(out, in_, scale, bias, *deps, fn=None):
+        fn = fn or (COPY if isinstance(bias, float) else FN.Identity)
+        return do("s", lambda: S.activation(out, in_, fn, bias, scale), *deps)
+
+    def total(out, junk, in_, fn, *deps):
+        return do("s", lambda: S.activation(junk, in_, fn, accum_out=out), *deps)
 
     def iota(ap, pattern, base, cm=0, flag=True):
         if flag:
@@ -193,8 +200,11 @@ def rank_program(g, core, T, topo):
         return (RemoteDMATransfer(dst_ids=[dest(topo, core, c) for c in to], dma_engine_mask=eng(topo, core, to[0], ab[0], ab[1]),
                                   remote_sem=T.sem[sem], srcs=[src], dsts=[dst] * len(to)), ab[1] - ab[0])
 
-    def send_cross(buf, rbuf, sem, *deps):
-        send([xfer(view(T, buf, 64 * i, 64 * i + 64), view(T, rbuf, 0, 64), [k], HAND[i], sem) for i, k in enumerate(relays)], *deps)
+    def send_cross(k, pc, ps):
+        send([xfer(view(T, "slot%sc" % k, 64 * i, 64 * i + 64), view(T, "r%sc" % k, 0, 64), [r], HAND[i], "rc" + k) for i, r in enumerate(relays)], pc)
+        at = 32 * pair.index(me)
+        send([xfer(T["slot%ss" % k][:, 32 * i:32 * i + 32], T["r%ss" % k][:, at:at + 32], [relays_all[pair[i % 2]][i // 2]], (4 * i, 4 * i + 4), "rs" + k)
+              for i in range(4)], ps)
 
     def send_same(buf, land, sem, *deps):
         tr, at = [], 32 * me
@@ -220,10 +230,14 @@ def rank_program(g, core, T, topo):
     i_p = iota(T.pb[:, 0:2], [[-AT, 2]], AT, 1, False)
     i_t = iota(T.pt[:], steps, pos[0])
     i_r = iota(T.r2[:], [[0, 8], [1, 16], [16, 2]], 128)
-    i_1 = iota(T.r1[:], [[0, 8], [1, 16], [0, 2]], 0)
-    iota(T.v16[:], [[1, 8], [128, 2]], 0)
-    i_c = iota(T.c128[:], [[128, 8]], -AT)
+    iota(T.pf[:, 0:1], [[1, 1]], 1, 2)
+    i_f = iota(T.pf[:, 1:2], [[1, 1]], 256 * (CAPP - 1) + 127, -1)
+    iota(T.r1[:], [[0, 8], [1, 16]], 0)
+    iota(T.v16[:], [[1, 8], [128, 2], [0, 2]], 0)
+    iota(T.rf[:], [[1, 8], [0, 2]], 0)
+    i_c = iota(T.c128[:], [[128, 8]], 0)
     c_x = vset(T.xh[:, 0:8], 0.0)
+    vset(T.pf[:, 3:4], 127.0 + CAPP)
     c_tx = vset(T.tx[:], 99.0)
     c_t2 = vset(T.t2x[:], 99.0)
     vset(T.t1[:, 34:544:4], 0.0)
@@ -233,7 +247,7 @@ def rank_program(g, core, T, topo):
     ts(T.pb[:, 2:4], T.pb[:, 0:2], 240, None, OP.bitwise_and, None, i_p)
     ts(T.pb[:, 4:6], T.pb[:, 0:2], 15, None, OP.bitwise_and, None)
     c_m = tt(T.t1[:, 32:544:4], T.tm[:, 0:128], T.tm[:, 128:256], OP.add, h)
-    ts(T.pb[:, 6:7], T.pb[:, 1:2], 4, None, OP.logical_shift_right, None)
+    ts(T.pb[:, 6:7], T.pb[:, 1:2], 31, None, OP.bitwise_and, None)
     h = ts(T.pb[:, 7:8], T.pb[:, 1:2], 1, None, OP.bitwise_and, None)
     for b in range(2):
         h2 = vset(T.c3[:, 264 * b:264 * b + 8], BIG, c_c3)
@@ -244,14 +258,14 @@ def rank_program(g, core, T, topo):
     c_m2 = lin(T.m2[:, 1:256:2], T.t1[:, 32:544:4], -1.0, 0.0)
     for k in (0, 3):
         c_t22 = act(T.t2x[:, k:32:4], T.pt[:], i_t, c_t2)
-    for k in (1, 2, 5, 265, 268):
+    for k in (2, 5, 268):
         c_s3 = lin(T.c3[:, k:k + 1], T.i8[:, 0:1], 0.0, 0.0, h2)
     col = [T.pbh[:, i:i + 1] for i in range(10)]
-    rho, odd = col[5], col[7]
+    rho = col[5]
 
     xq = do("v", lambda: V.quantize_mx(T.xq[:], T.xs[:], T.xh[:]), ldx, ldp, c_x)
-    z = mm(T.z, 128, T.xq, T.xs, AT, 0, xq)
-    c_om = ts(T.ofm[:, 0:1], odd, 8.0, col[6], OP.mult, OP.add, c_pb)
+    z = mm(T.z, 134, T.xq, T.xs, AT, 0, xq)
+    c_dm = ts(T.dm[:], T.dd[:], 0.0, 0.9375, OP.is_equal, OP.mult)
     for b in range(2):
         c_c3 = ts(T.c3[:, 264 * b + 8:264 * b + 264:2], T.dd[:], 0.0, BIG, OP.is_lt, OP.mult)
     b0, b1, b2 = [T.bt[:, i:i + 1] for i in range(3)]
@@ -262,49 +276,52 @@ def rank_program(g, core, T, topo):
     hb = ts(T.bk[:, 0:1], b1, b2, 2.0, OP.add, OP.mult)
     cn = count("1", T.t1, 8, T.cn, h)
     h = ts(T.bk[:, 1:2], T.bk[:, 0:1], b0, None, OP.add, None, hb)
+    hz = tt(T.pd[:, 0:128], T.z[:, AT:AT + 128], T.dm[:], OP.mult)
     for k in range(2):
         ts(T.t2[:, k:64:2], T.t2x[:], T.bk[:, 1:2], col[2 + 2 * k], OP.is_equal, OP.mult, h, c_t22)
+    hb = lin(T.sg[:, 1:2], T.bk[:, 1:2], 256.0 * CAPP, T.pf[:, 1:2], h, i_f)
+    hz = total(T.sg[:, 0:1], T.junk[:, 0:128], T.pd[:, 0:128], FN.Sign, hz)
     h = red(T.key[:, 0:1], T.cn[:, 0:8], OP.max, cn)
     for k in range(2):
         h2 = ts(T.t2[:, 64 + k:576:2], T.r2[:], T.key[:, 0:1], None, OP.is_equal, None, h, i_r)
+    hb = lin(T.sg[:, 2:3], T.sg[:, 0:1], T.pf[:, 0:1], T.sg[:, 1:2], hb, hz)
+    hv = lin(T.vv[:, 0:1], T.key[:, 0:1], -1.0, T.pf[:, 3:4], h, fn=FN.Relu)
+    ms = ts(T.ms[:, 0:1], T.vv[:, 0:1], -256.0, T.sg[:, 2:3], OP.mult, OP.add, hv)
+    send([xfer(T.ms[:, 0:1], T.rm1[:], relays, MSG["relay"], "rn1")], ms, i_c)
+    note_same(T.ms[:, 0:1], "nl1", "n1")
     lp = count("2", T.t2, 16, T.lp, h2)
-    c_dm = ts(T.dm[:], T.dd[:], 0.0, 0.9375, OP.is_equal, OP.mult)
     ts(T.tri[:, 0:128], T.dd[:, 127::-1], 0.0, BIG, OP.is_lt, OP.mult)
+    c_tri = vset(T.tri[:, 128:256], BIG)
     XQ, L1 = ("xq", "xs"), ("land1c", "land1s")
     o1 = vcopy(T.off1[:], T.lp[:, 0:16], lp)
-    lb = vcopy(T.lb[:], T.lp[:, 0:16])
     pk = [pick("slot1", XQ, 134, 128 * e, 128 * e + 128, T.off1[:, 8 * e:8 * e + 8], o1) for e in range(2)]
-    send_cross("slot1c", "r1c", "rc1", pk[0][0])
-    send_cross("slot1s", "r1s", "rs1", pk[0][1])
+    send_cross("1", *pk[0])
     send_same("slot1c", "land1c", "a1", pk[1][0])
     send_same("slot1s", "land1s", "a1", pk[1][1])
     i = pos.index(me)
     own1 = pick("land1", XQ, 134, 32 * me, 32 * me + 32, T.off1[:, 2 * i:2 * i + 2], o1)
 
-    e0, p0 = pos.index(0) // 4, 32 * (pos.index(0) % 4)
-    zz = mm(T.z, 128, T.slot1c, T.slot1s, 128 * e0, 128 * e0, h1, *pk[e0])
-    m1 = act(T.m1[:], T.lb[:].indirect(T.ofm[:, 0:1]), lb, c_om)
-    h = ts(T.sg[p0:p0 + 1, 0:1], T.z[p0:p0 + 1, p0:p0 + 1], 0.0, 2.0, OP.is_gt, OP.mult, zz)
-    h2 = vcopy(T.ms[:], T.m1[:, 0:2], m1)
-    m1 = ts(T.ms[p0:p0 + 1, e0:e0 + 1], T.sg[p0:p0 + 1, 0:1], -1.0, T.m1[p0:p0 + 1, e0:e0 + 1], OP.add, OP.mult, h, h2)
-    note_out(T.ms[:, 0:1], "rm1", "rn1", m1)
-    note_same(T.ms[:, 1:2], "nl1", "n1")
-
     load("y", "ldz", T.land3c[:, 256:258].bitcast(dt.uint8), T.xq[:, 0:2].bitcast(dt.uint8), xq)
     ldz = load("y", "ldz", T.land3s[:, 256:258], T.xs[:, 0:2], xq)
-    c_tri = vset(T.tri[:, 128:256], BIG)
-    own_n = vcopy(T.nl1[:, 8 * me:8 * me + 1], T.ms[:, 1:2], m1)
-    lin(T.nb[:], T.r2[:], 0.0, 0.0, i_r)
+    own_n = vcopy(T.nl1[:, 8 * me:8 * me + 1], T.ms[:, 0:1], ms)
+    c_rep = vcopy(T.rep[:], T.rf[:], i_c)
+    vset(T.t3[:], 0.0)
+    h5 = lin(T.rb[:], T.r2[:], 0.0, 0.0, i_r)
+    lin(T.pf[:, 2:3], col[6], -256.0, -256.0 * CAPP * me - 128.0, c_pb)
+    lin(T.nb[:], T.r2[:], 0.0, 0.0)
+    lin(T.rb[:, 0:256:32], T.i8[:], 0.0, BIG, h5)
     lin(T.nf[:], T.r2[:], 0.0, 0.0)
     for k in range(2):
         for j in range(2):
             h = lin(T.kv[:, 16 * j + k:16 * j + 16:2], T.pt[:], 2.0, 4096.0 + k)
+    if me == 0:
+        vset(T.wa[:], 0.0)
     for a in range(4):
         for k in range(4):
             h2 = vset(quad("kv", a, slice(32 + k, 64, 4)), 4096.0 + 2 * pos[4 * (k // 2) + a] + k % 2)
     lin(T.one[:], T.i8[:], 0.0, 1.0)
     h3 = lin(T.rst9[:], T.r2[:, 0:72], 0.0, 1.0)
-    lin(col[8], col[3], 1.0, 128.0, c_pb)
+    lin(col[8], col[3], 1.0, 128.0)
     h4 = lin(T.k8[:], rho, 16.0, 2.0 * me)
     lin(T.nft[:, 256:264], T.i8[:], 0.0, -1.0)
     lin(T.rst9[:, 0:72:9], T.i8[:], 0.0, 0.0, h3)
@@ -312,102 +329,118 @@ def rank_program(g, core, T, topo):
     c_s = lin(T.it[:, 0:72:9], T.i8[:], 256.0, T.k8[:, 0:1])
     c_w = do("v", lambda: V.quantize_mx(T.wq[:], T.ws[:], T.wh[:]), ldw)
     h = turn(T.kt[:], T.kv[:], h, h2)
-    vcopy(T.kk[:], T.kt[:, 0:64:32], h)
-    c_k = ts(T.kq[:], T.kt[:, 0:64:32], -7.5, None, OP.add, None)
+    vcopy(T.kk[:, 0:2], T.kt[:, 0:64:32], h)
+    c_k = ts(T.kk[:, 2:4], T.kt[:, 0:64:32], -7.5, None, OP.add, None)
 
     a1, n1 = ("a1", 2 * ncol), ("n1", nmsg)
+    h = vcopy(T.nlf[:], T.nl1[:, 0:64:8], n1, own_n)
+    rp = act(T.rp[:], T.nlf[:].indirect(T.rep[:]), h, c_rep)
+    if me == 0:
+        h = ts(T.wa[:, 0:8], T.nlf[:], -1.0, 256.0, OP.mult, OP.add, h)
+        h = turn(T.wb[:, 0:32], T.wa[:, 0:32], h)
+        h = red(T.wa[:, 32:33], T.wb[:, 0:32], OP.max, h)
+        h = turn(T.wb[:, 32:64], T.wa[:, 32:64], h)
+        for a in range(4):
+            w4 = cast(T.wc[:, 8 * a:8 * a + 8], T.wb[32 * a:32 * a + 1, 32:40], h)
+    h = turn(T.rt[:], T.rp[:], rp)
+    ab = lin(T.ab[:], T.rt[:], 1.0, T.pf[:, 2:3], h, c_s, fn=FN.Abs)
+
     gs = [T.ga, T.gb]
     wd = [(slice(128 * b, 128 * b + 128), slice(128 * b, 128 + 256 * b), 128 + 128 * b) for b in range(2)]
     gm = [mm(gs[b], wd[b][2], T.land1c, T.land1s, 128 * b, 0, a1, *own1) for b in range(2)]
-    if me == 0:
-        n8 = cast(T.n8[:], T.nl1[32 * am:32 * am + 1, 0:64:8], n1, own_n)
     mx, th = [], []
     for b in range(2):
         w, w2, n = wd[b]
-        h = tt(T.pd[:, w], gs[b][:, w], T.dm[:], OP.mult, gm[b], c_dm)
-        th.append(do("s", lambda: S.activation(T.junk[:, w], T.pd[:, w], COPY, accum_out=T.thr[:, b:b + 1]), h))
-        mx.append(do("v", lambda: V.tensor_tensor_scan(T.xg[:, w2], gs[b][:, n - 1::-1], T.tri[:, 0:n], 0.0, OP.max, OP.min), c_tri))
+        h = tt(T.pd[:, w], gs[b][:, w], T.dm[:], OP.mult, gm[b], hz)
+        th.append(total(T.thr[:, b:b + 1], T.junk[:, w], T.pd[:, w], COPY, h))
+        mx.append(scan(T.xg[:, w2], gs[b][:, n - 1::-1], T.tri[:, 0:n], c_tri, ops=(OP.max, OP.min)))
     for b in range(2):
         at = 128 * b + wd[b][2] - 1
-        t3 = ts(T.t3[:, b:528:2], T.c3[:, 264 * b:264 * b + 264], T.xg[:, at:at + 1], T.thr[:, b:b + 1], OP.add, OP.is_lt, mx[b], th[b], c_c3, c_s3)
+        if me == 0 and b:
+            w4 = tt(T.wc[:, 32:48], T.wc[:, 0:16], T.wc[:, 16:32], OP.max, w4)
+        t3 = ts(T.t3[:, b:512:4], T.c3[:, 528:656], T.xg[:, at:at + 1], T.thr[:, b:b + 1], OP.add, OP.is_lt, mx[b], th[b], c_c3)
     if me == 0:
-        ts(T.em[:], T.n8[:], 0.0, None, OP.is_equal, None, n8)
-        h = ts(T.ng[:], T.n8[:], 0.0, None, OP.is_lt, None)
-    sp = count("3", T.t3, 4, T.sp, t3)
+        w4 = tt(T.wc[:, 48:56], T.wc[:, 32:40], T.wc[:, 40:48], OP.max, w4)
+    sp = count("3", T.t3, 0, T.sp, t3)
     size = T.cl[:, 8 * me:8 * me + 1]
-    qd = ts(T.qd[:], T.t3[:, 2:4], -257.0, 256.0, OP.mult, OP.add)
     if me == 0:
-        he = scan(T.ee[:], T.em[:, 7::-1], T.ng[:, 7::-1], h)
-        hn = lin(T.na[:], T.nl1[:, 0:64:8], 1.0, 0.0, n1, own_n)
-        hn = do("s", lambda: S.activation(T.na[:], T.na[:], ActivationFunctionType.Abs), hn)
-        nb = tt(T.nb[:, 0:256:32], T.na[:], T.c128[:], OP.add, hn, c_s, i_c)
-        sz = ts(size, T.sp[:, 0:1], T.ee[:, 7:8], 2.0, OP.add, OP.mult, sp, he)
+        ts(T.en[:, 0:8], T.wc[:, 48:56], 0.0, None, OP.is_le, None, w4)
+        h = ts(T.en[:, 8:16], T.wc[:, 48:56], 128.0, None, OP.is_gt, None)
+    for b in range(2):
+        t5 = ts(T.t5[:, b:528:2], T.c3[:, 264 * b:264 * b + 264], 0.5, T.t3[:, b:b + 1], OP.is_lt, OP.mult, c_s3)
+        if me == 0 and b == 0:
+            he = scan(T.en[:, 16:24], T.en[:, 7::-1], T.en[:, 15:7:-1], h)
+    if me == 0:
+        sz = ts(size, T.sp[:, 0:1], T.en[:, 23:24], 2.0, OP.add, OP.mult, sp, he)
     else:
-        nb = tt(T.nb[:, 0:256:32], T.nl1[:, 0:64:8], T.c128[:], OP.add, n1, own_n, c_s, i_c)
         sz = ts(size, T.sp[:, 0:1], 2.0, None, OP.mult, None, sp)
 
     note_out(size, "rm2", "rn2", sz)
     note_same(size, "cl", "c2")
-    h = tt(T.ti[:], T.sp[:, 1:3], T.qd[:], OP.add, qd)
-    nt = turn(T.nt[:], T.nb[:], nb)
-    nw = cast(T.nw[:], T.nt[32 * am:32 * am + 1, :], nt)
+    cu = count("5", T.t5, 4, T.cn, t5)
+    qd = ts(T.qd[:], T.t3[:, 0:2], -257.0, 256.0, OP.mult, OP.add)
+    sm = scan(T.sm[:], T.rb[:], T.ab[:], ab, ops=(OP.add, OP.min))
+    h = tt(T.ti[:], T.cn[:, 1:3], T.qd[:], OP.add, qd, cu)
+    hq = [(vcopy if a % 2 else act)(T.mq[0:32, a:32:4], quad("sm", a, slice(31, 256, 32)), sm) for a in range(4)]
     ts(T.uv[:, 0:2], T.ti[:], 3, 15, OP.logical_shift_right, OP.bitwise_and, h)
     h = ts(T.uv[:, 2:4], T.ti[:], 256 + 128 + 7, None, OP.bitwise_and, None)
     if me == 0:
-        he = ts(T.e2[:], T.ee[:, 7:8], 2.0, None, OP.mult, None)
+        he = ts(T.e2[:], T.en[:, 23:24], 2.0, None, OP.mult, None)
+    hm = scan(T.mr[0:32, :], T.rb[0:32, 0:256:8], T.mq[0:32, :], *hq, ops=(OP.add, OP.min))
     h = vcopy(T.uvf[:], T.uv[:], h)
+    hm = tt(T.nb[0:32, 0:256:32], T.mr[0:32, 3:32:4], T.c128[0:32, :], OP.add, hm)
+    for a in range(1, 4):
+        nb = act(quad("nb", a, slice(0, 256, 32)), T.nb[0:32, 0:256:32], hm)
     for b in range(2):
+        ts(T.t4[:, b:64:2], T.v16[:], T.uvf[:, 2 + b:3 + b], None, OP.is_equal, None, h)
         for k in range(2):
-            ts(T.t4[:, b + 2 * k:64:4], T.v16[:], T.uvf[:, 2 + b:3 + b], rho if k else col[8 if b else 3], OP.is_equal, OP.mult, h)
-    for b in range(2):
-        h2 = ts(T.t4[:, 64 + b:576:2], T.r1[:], T.uvf[:, b:b + 1], None, OP.is_equal, None)
+            h2 = ts(T.t4[:, 64 + b + 2 * k:576:4], T.r1[:], T.uvf[:, b:b + 1], rho if k else col[8 if b else 3], OP.is_equal, OP.mult)
     pp = count("4", T.t4, 16, T.pp, h2)
+    nw = turn(T.nw[:], T.nb[:], nb)
     plw = act(T.plw[:], T.pp[:, 0:16], pp)
 
     c2 = ("c2", nmsg)
     if me:
         he = end = scan(T.end[:], T.one[:], T.cl[:, 0:64:8], c2, sz)
     before = T.end[:, me - 1:me] if me else T.e2[:, 0:1]
-    ts(T.vi[:], T.kq[:], before, 0.0625, OP.subtract, OP.mult, he, c_k)
-    h = ts(T.vx[:], T.kk[:], before, None, OP.subtract, None)
+    ts(T.vi[:], T.kk[:, 2:4], before, 0.0625, OP.subtract, OP.mult, he, c_k)
+    h = ts(T.vx[:], T.kk[:, 0:2], before, None, OP.subtract, None)
     if me:
         hd = ts(T.d256[:], T.cl[:, 0:64:8], -1.0, 512.0, OP.mult, OP.add)
     ov = [ts(T.ov[:, 2 * k:2 * k + 1], T.vi[:, k:k + 1], -16.0, T.vx[:, k:k + 1], OP.mult, OP.add, h) for k in range(2)]
     o3 = vcopy(T.off3[:], T.plw[:].indirect(T.ov[:, 0:1]), ov[0], plw)
     on = vcopy(T.offn[:], T.plw[:].indirect(T.ov[:, 2:3]), ov[1])
-    pc, ps = pick("slot3", L1, 256, 0, 128, T.off3[:, 0:8], o3, a1, *own1)
-    send_cross("slot3c", "r3c", "rc3", pc)
-    send_cross("slot3s", "r3s", "rs3", ps)
+    send_cross("3", *pick("slot3", L1, 256, 0, 128, T.off3[:, 0:8], o3, a1, *own1))
     n3 = act(T.n3[:], T.nw[:].indirect(T.offn[:, 0:4]), on, nw)
     pc, ps = pick("slot3", L1, 256, 128, 256, T.off3[:, 8:16], o3)
     h = turn(T.nt3[:], T.n3[:], n3)
     hc = pickc(T.land3c[:, 32 * me:32 * me + 32], T.land1c[:], T.off3[:, 2 * i:2 * i + 2])
     m3 = vcopy(T.m3[:], T.nt3[:, 0:64:32], h)
     own3 = (hc, act(T.land3s[:, 32 * me:32 * me + 32], T.land1s[:].indirect(T.off3[:, 2 * i:2 * i + 2])))
-    send_same("slot3c", "land3c", "a3", pc)
     note_out(T.m3[:, 0:1], "rm3", "rn3", m3)
+    send_same("slot3c", "land3c", "a3", pc)
     send_same("slot3s", "land3s", "a3", ps)
     note_same(T.m3[:, 1:2], "nl3", "n3")
     own_n3 = vcopy(T.nl3[:, 8 * me:8 * me + 1], T.nt3[:, 32:33])
 
     if me == 0:
-        h = ts(T.nk8[:], T.n8[:], 0.0, -1.0, OP.min, OP.mult)
         ts(T.it[:, 0:72:9], T.gg[:], T.e2[:, 0:1], None, OP.subtract, None)
-        h = tt(T.nk[:], T.nk8[:], T.c128[:], OP.add, h)
+        h = tt(T.nk[:, 0:8], T.nw[:, 0:256:32], T.en[:, 8:16], OP.mult, nw)
         end = scan(T.end[:], T.one[:], T.cl[:, 0:64:8], c2)
-        h = ts(T.nk8[:], T.nk[:], 1.0, None, OP.add, None, h)
         hd = ts(T.d256[:], T.cl[:, 0:64:8], -1.0, 512.0, OP.mult, OP.add)
-        h = tt(T.nk[:], T.nk8[:], T.ng[:], OP.mult, h)
+        nk = scan(T.nk[:, 8:16], T.en[:, 7::-1], T.nk[:, 7::-1], h)
         hd = ts(T.d256[:, 0:1], T.d256[:, 0:1], T.e2[:, 0:1], None, OP.add, None, hd)
-        nk = scan(T.nk8[:], T.em[:, 7::-1], T.nk[:, 7::-1], h)
     for d in range(N):
         h2 = ts(T.it[:, 1 + d:72:9], T.gg[:], T.end[:, d:d + 1], T.d256[:, d:d + 1], OP.is_ge, OP.mult, hd, end)
     h = scan(T.its[:], T.rst9[:], T.it[:], h2)
     if me == 0:
-        nk = ts(T.nk[:, 0:1], T.nk8[:, 7:8], -1.0, None, OP.add, None, nk)
+        ts(T.nft[:, 257:258], T.nk[:, 15:16], -1.0, None, OP.add, None, nk)
     h = vcopy(T.xi[:], T.its[:, 8:72:9], h)
     h = ts(T.xsh[:], T.xi[:], 4, None, OP.logical_shift_right, None, h)
     oz = ts(T.offz[:], T.xsh[:], 256.0, None, OP.min, None, h)
+    if me == 0:
+        h = ts(T.nk[:, 16:17], T.xsh[:, 0:1], 1.0e6, None, OP.is_gt, None)
+        oz = ts(T.offz[:, 0:1], T.xsh[:, 0:1], 256.0, T.nk[:, 16:17], OP.min, OP.add, h)
 
     a3 = ("a3", 2 * ncol)
     fc = pickc(T.fq[:], T.land3c[:], T.offz[:], a3, ldz, oz, *own3)
@@ -416,12 +449,10 @@ def rank_program(g, core, T, topo):
     load("y", "dout", T.oc[:], T.fq[:].bitcast(dt.uint8), fc)
     h = vcopy(T.nf[:, 0:256:32], T.nl3[:, 0:64:8], ("n3", nmsg), own_n3)
     h = turn(T.nft[:, 0:256], T.nf[:], h)
-    no = vcopy(T.no[:], T.nft[:].indirect(T.offz[:]), h)
-    if me == 0:
-        no = ts(T.no[:, 0:1], T.no[:, 0:1], T.nk[:, 0:1], None, OP.max, None, no, nk)
     for k in range(4):
         load("y", "dout", T.osc[4 * k:4 * k + 4, :], T.fs[32 * k:32 * k + 4, :], fs)
     ys = act(T.ysb[:], T.yp[:, 0:128], yp)
     load("s", "dout", T.y[:], T.ysb[:], ys)
+    no = vcopy(T.no[:], T.nft[:].indirect(T.offz[:]), h)
     load("y", "dout", T.num[:], T.no[32 * am:32 * am + 1, :], no)
     wait("p", [(s, cnt[s]) for s in ("qv", "qs", "qt", "qp", "dout", "ls", "ldz", "ldp", "ldx", "ldw")])

@@ -7,19 +7,20 @@ COPY = FN.Copy
 X = AxisListType.X
 N, P, L, CAPP = 8, 128, 3, 32
 BIG = 1.0e29
+WHOLE = 1.5 * 2 ** 23
 AT = 6
 
 SCRATCH = {}
 for _kind, _list in {
     "bfloat16": "xh 536 wh 512 dd 128 tm 256 m2 256 tx 32 t2x 32 r2 256 r1 128 t1 544 t2 576 t3 512 t5 528 t4 576 c3 656 "
-                "one 8 cl 64 rm2 1 pbh 10 bt 4 bk 2 key 2 uvf 4 v16 32 vv 2",
+                "one 16 cl 72 rm2 1 pbh 10 bt 4 bk 2 key 2 uvf 4 v16 32 szb 2 nb 256 nj 256",
     "float8_e4m3fn_x4": "xq 134 wq 128 q1 136 q2 144 q3 128 q5 132 q4 144 slot1c 256 land1c 256 slot3c 256 land3c 258 fq 128 r1c 64 r3c 64",
     "uint8": "xs 134 ws 128 s1 136 s2 144 s3 128 s5 132 s4 144 slot1s 256 land1s 256 slot3s 256 land3s 258 fs 128 r1s 64 r3s 64",
-    "uint16": "rep 16 ms 2 nl1 64 rm1 1 off1 16 ov 4 off3 16 offn 16 nl3 64 m3 2 offz 8 rm3 1",
-    "int32": "pb 8 ti 2 uv 4 vi 2 xi 8 xsh 8",
-    "float32": "i8 8 pt 8 rst9 72 c128 8 gg 8 k8 1 dm 128 tri 256 kv 64 kt 64 kk 4 vx 2 pd 256 thr 2 xg 384 "
-               "nb 256 nw 256 qd 2 plw 16 n3 64 nt3 64 end 8 d256 8 it 72 its 72 nf 256 nft 264 no 128 ysb 128 "
-               "en 24 e2 1 nk 24 junk 256 pf 4 sg 4 nlf 8 rp 256 rt 256 ab 256 rb 256 sm 256 mq 32 mr 32 wa 64 wb 64 wc 64 rf 16",
+    "uint16": "rep 16 ms 2 nl1 16 nlx 6 rm1 1 off1 16 ov 4 off3 16 offn 16 nl3 64 m3 2 offz 8 rm3 1",
+    "int32": "pb 8 ti 2 uv 4 vi 2 xsh 8",
+    "float32": "i8 8 pt 8 rst9 72 kc 16 dz 128 sq 64 gg 8 dm 128 tri 256 kv 64 kt 64 kk 4 kq 32 vx 4 pd 256 thr 2 xg 384 "
+               "qd 2 plw 16 n3 64 nt3 64 end 9 d256 9 it 72 its 72 nf 256 nft 264 no 128 ysb 128 "
+               "en 97 nk 128 junk 256 pf 5 sg 2 nlf 8 rp 256 rt 256 ab 256 rb 256 sm 256 mq 32 mr 32 wa 96 wb 64 wc 32 rf 16",
 }.items():
     _w = _list.split()
     for _i in range(0, len(_w), 2):
@@ -27,7 +28,7 @@ for _kind, _list in {
 for _n in ("z", "cn", "lp", "ga", "gb", "sp", "pp", "yp"):
     SCRATCH[_n] = ("psum", [128, 512], "float32")
 SEMAPHORES = ["qv", "qs", "qt", "qp", "ldp", "ldx", "ldw", "ldz", "dout", "ls",
-              "a1", "n1", "c2", "a3", "n3", "rc1", "rs1", "rn1", "rn2", "rc3", "rs3", "rn3"]
+              "a1", "n1", "n1x", "c2", "a3", "n3", "rc1", "rs1", "rn1", "rn2", "rc3", "rs3", "rn3"]
 
 
 def wiring(T, topo):
@@ -60,7 +61,12 @@ def view(T, buf, a, b):
     return v.bitcast(dt.uint8) if buf[-1] == "c" else v
 
 
-def relay_program(g, core, T, topo, s, group, first, one):
+def seat(T, land, s, r):
+    at = 8 * (s + (land == "cl" and s > r))
+    return T[land][:, at:at + 1]
+
+
+def relay_program(g, core, T, topo, s, group, first, one, at):
     to = [T.cores[r] for r in group]
     sent = [0]
 
@@ -72,19 +78,19 @@ def relay_program(g, core, T, topo, s, group, first, one):
     def write(d, a, b, rsem, src, dst):
         return RemoteDMATransfer(dst_ids=[dest(topo, core, d)], dma_engine_mask=eng(topo, core, d, a, b), remote_sem=T.sem[rsem], src=src, dst=dst)
 
-    def cols(k):
-        go("rc" + k, [write(d, 4 * i, 4 * i + 4, "a" + k, view(T, "r%sc" % k, 32 * i, 32 * i + 32), view(T, "land%sc" % k, 32 * s, 32 * s + 32))
-                      for i, d in enumerate(to)])
-        go("rs" + k, [write(T.cores[one], 0, 8, "a" + k, T["r%ss" % k][:], T["land%ss" % k][:, 32 * first:32 * first + 64])])
+    def both(sem, buf, land, rsem):
+        go(sem, [write(T.cores[one], 0, 8, rsem, view(T, buf, 0, 64), view(T, land, 32 * first, 32 * first + 64))])
 
     def note(sem, src, land, rsem):
         go(sem, [RemoteDMATransfer(dst_ids=[dest(topo, core, d) for d in to], dma_engine_mask=eng(topo, core, to[0], 0, 8), remote_sem=T.sem[rsem],
-                                   srcs=[T[src][:]], dsts=[T[land][:, 8 * s:8 * s + 1]] * 2)])
+                                   srcs=[T[src][:]], dsts=[seat(T, land, s, r) for r in group])])
 
-    note("rn1", "rm1", "nl1", "n1")
-    cols("1")
+    go("rn1", [write(to[0], 0, 8, "n1x", T.rm1[:], T.nlx[:, at:at + 1])])
+    both("rc1", "r1c", "land1c", "a1")
+    both("rs1", "r1s", "land1s", "a1")
     note("rn2", "rm2", "cl", "c2")
-    cols("3")
+    go("rc3", [write(d, 4 * i, 4 * i + 4, "a3", view(T, "r3c", 32 * i, 32 * i + 32), view(T, "land3c", 32 * s, 32 * s + 32)) for i, d in enumerate(to)])
+    both("rs3", "r3s", "land3s", "a3")
     note("rn3", "rm3", "nl3", "n3")
     g.wait_ge(T.sem.ls, sent[0])
 
@@ -96,15 +102,16 @@ def rank_program(g, core, T, topo):
         for s in range(N):
             if core in relays_all[s]:
                 i = relays_all[s].index(core)
-                relay_program(g, core, T, topo, s, cross_all[s][2 * i:2 * i + 2], pair_all[s][0], cross_all[s][2 * i + pair_all[s].index(s)])
+                relay_program(g, core, T, topo, s, cross_all[s][2 * i:2 * i + 2], pair_all[s][0], cross_all[s][2 * i + pair_all[s].index(s)],
+                              same_all[s].index(s))
         return
     same, cross, relays, pair = same_all[me], cross_all[me], relays_all[me], pair_all[me]
     pos = cross + same
-    steps = [[pos[k] - pos[0], 2] for k in (4, 2, 1)]
-    assert pos == [pos[0] + sum(steps[b][0] * (i >> 2 - b & 1) for b in range(3)) for i in range(N)]
-    am = same.index(me)
+    assert pos == [pos[0] + sum((pos[k] - pos[0]) * (i // k % 2) for k in (4, 2, 1)) for i in range(N)]
+    am, ap = same.index(me), pair.index(me)
     peer = [r for r in pair if r != me]
     far = [r for r in same if r not in pair]
+    came = cross + far + pair
     ncol = 8 * len(peer) + 4 * len(far) + 4 * len(cross)
     nmsg = 8 * (N - 1)
 
@@ -151,8 +158,8 @@ def rank_program(g, core, T, topo):
     def red(out, in_, op, *deps):
         return do("v", lambda: V.tensor_reduce(out, in_, X, op), *deps)
 
-    def scan(out, d0, d1, *deps, ops=(OP.mult, OP.add)):
-        return do("v", lambda: V.tensor_tensor_scan(out, d0, d1, 0.0, *ops), *deps)
+    def scan(out, d0, d1, *deps, ops=(OP.mult, OP.add), init=0.0):
+        return do("v", lambda: V.tensor_tensor_scan(out, d0, d1, init, *ops), *deps)
 
     def turn(out, in_, *deps):
         return do("v", lambda: V.transpose(out, in_), *deps)
@@ -160,20 +167,14 @@ def rank_program(g, core, T, topo):
     def act(out, in_, *deps):
         return do("s", lambda: S.activation(out, in_, COPY), *deps)
 
-    def lin(out, in_, scale, bias, *deps, fn=None):
+    def lin(out, in_, scale, bias, *deps, fn=None, sum_to=None):
         fn = fn or (COPY if isinstance(bias, float) else FN.Identity)
-        return do("s", lambda: S.activation(out, in_, fn, bias, scale), *deps)
-
-    def total(out, junk, in_, fn, *deps):
-        return do("s", lambda: S.activation(junk, in_, fn, accum_out=out), *deps)
+        return do("s", lambda: S.activation(out, in_, fn, bias, scale, accum_out=sum_to), *deps)
 
     def iota(ap, pattern, base, cm=0, flag=True):
         if flag:
             return do("p", lambda: g.iota(ap, pattern, base, cm, allow_small_or_imprecise_dtypes=True))
         return do("p", lambda: g.iota(ap, pattern, base, cm))
-
-    def cast(out, in_, *deps):
-        return do("p", lambda: g.partition_broadcast(out, in_, 128), *deps)
 
     def mm(out, n, q, s, a, b, *deps):
         return do("t", lambda: E.matmul_mx(out[:, 0:n], q[:, a:a + 128], s[:, a:a + 128], q[:, b:b + n], s[:, b:b + n], True, True), *deps)
@@ -196,31 +197,29 @@ def rank_program(g, core, T, topo):
         g.remote_dma_fused([t for t, n in tr], local_sem=T.sem.ls)
         cnt["ls"] = cnt.get("ls", 0) + sum(n for t, n in tr)
 
-    def xfer(src, dst, to, ab, sem):
+    def xfer(src, dsts, to, ab, sem):
         return (RemoteDMATransfer(dst_ids=[dest(topo, core, c) for c in to], dma_engine_mask=eng(topo, core, to[0], ab[0], ab[1]),
-                                  remote_sem=T.sem[sem], srcs=[src], dsts=[dst] * len(to)), ab[1] - ab[0])
+                                  remote_sem=T.sem[sem], srcs=[src], dsts=dsts), ab[1] - ab[0])
 
-    def send_cross(k, pc, ps):
-        send([xfer(view(T, "slot%sc" % k, 64 * i, 64 * i + 64), view(T, "r%sc" % k, 0, 64), [r], HAND[i], "rc" + k) for i, r in enumerate(relays)], pc)
-        at = 32 * pair.index(me)
-        send([xfer(T["slot%ss" % k][:, 32 * i:32 * i + 32], T["r%ss" % k][:, at:at + 32], [relays_all[pair[i % 2]][i // 2]], (4 * i, 4 * i + 4), "rs" + k)
-              for i in range(4)], ps)
+    def send_two(buf, rbuf, sem, *deps):
+        send([xfer(view(T, buf, 64 * i, 64 * i + 64), [view(T, rbuf, 0, 64)], [r], HAND[i], sem) for i, r in enumerate(relays)], *deps)
+
+    def send_four(buf, rbuf, sem, *deps):
+        send([xfer(view(T, buf, 32 * i, 32 * i + 32), [view(T, rbuf, 32 * ap, 32 * ap + 32)], [relays_all[pair[i % 2]][i // 2]], (4 * i, 4 * i + 4), sem)
+              for i in range(4)], *deps)
 
     def send_same(buf, land, sem, *deps):
         tr, at = [], 32 * me
         for i, r in enumerate(far + peer):
             a = 32 * pos.index(r)
-            tr.append(xfer(view(T, buf, a, a + 32), view(T, land, at, at + 32), [T.cores[r]], COL["peer" if r in peer else i], sem))
+            tr.append(xfer(view(T, buf, a, a + 32), [view(T, land, at, at + 32)], [T.cores[r]], COL["peer" if r in peer else i], sem))
         send(tr, *deps)
 
-    def note(src, land, sem, to, ab):
-        return xfer(src, T[land][:, 8 * me:8 * me + 1], [T.cores[r] for r in to], ab, sem)
-
     def note_out(src, rbuf, sem, *deps):
-        send([xfer(src, T[rbuf][:], [k], HAND[i], sem) for i, k in enumerate(relays)], *deps)
+        send([xfer(src, [T[rbuf][:]] * 2, relays, MSG["relay"], sem)], *deps)
 
     def note_same(src, land, sem, *deps):
-        send([note(src, land, sem, far, MSG["far"]), note(src, land, sem, peer, MSG["peer"])], *deps)
+        send([xfer(src, [seat(T, land, me, r) for r in to], [T.cores[r] for r in to], MSG[k], sem) for k, to in (("far", far), ("peer", peer))], *deps)
 
     ldp = load("y", "ldp", T.xh[:, 8:4 * AT], T.pl[:, 0:16])
     ldx = load("s", "ldx", T.xh[:, 4 * AT:536], T.x[:])
@@ -228,46 +227,36 @@ def rank_program(g, core, T, topo):
     i_d = iota(T.dd[:], [[1, 128]], 0, -1)
     i_8 = iota(T.i8[:], [[1, 8]], 0)
     i_p = iota(T.pb[:, 0:2], [[-AT, 2]], AT, 1, False)
-    i_t = iota(T.pt[:], steps, pos[0])
-    i_r = iota(T.r2[:], [[0, 8], [1, 16], [16, 2]], 128)
+    i_t = iota(T.pt[:], [[pos[k] - pos[0], 2] for k in (4, 2, 1)], pos[0])
     iota(T.pf[:, 0:1], [[1, 1]], 1, 2)
-    i_f = iota(T.pf[:, 1:2], [[1, 1]], 256 * (CAPP - 1) + 127, -1)
-    iota(T.r1[:], [[0, 8], [1, 16]], 0)
-    iota(T.v16[:], [[1, 8], [128, 2], [0, 2]], 0)
-    iota(T.rf[:], [[1, 8], [0, 2]], 0)
-    i_c = iota(T.c128[:], [[128, 8]], 0)
+    i_f = iota(T.pf[:, 1:2], [[1, 1]], 127 - 32768, -1)
+    i_r = iota(T.r2[:], [[0, 8], [256, 16], [4096, 2]], 32768)
+    iota(T.kq[:], [[0, 8], [2 * (pos[4] - pos[0]), 2], [1, 2]], 0)
+    i_v = iota(T.v16[:], [[1, 8], [128, 2], [0, 2]], 0)
     c_x = vset(T.xh[:, 0:8], 0.0)
-    vset(T.pf[:, 3:4], 127.0 + CAPP)
     c_tx = vset(T.tx[:], 99.0)
     c_t2 = vset(T.t2x[:], 99.0)
     vset(T.t1[:, 34:544:4], 0.0)
-    c_c3 = vset(T.c3[:], 0.0)
-    ts(T.tm[:, 0:128], T.dd[:], 0.0, 127.0, OP.is_equal, OP.mult, i_d)
-    h = ts(T.tm[:, 128:256], T.dd[:], 0.0, None, OP.is_ge, None)
-    ts(T.pb[:, 2:4], T.pb[:, 0:2], 240, None, OP.bitwise_and, None, i_p)
-    ts(T.pb[:, 4:6], T.pb[:, 0:2], 15, None, OP.bitwise_and, None)
+    ts(T.tm[:, 0:128], T.dd[:], 0.0, 127.0 * 256, OP.is_equal, OP.mult, i_d)
+    h = ts(T.tm[:, 128:256], T.dd[:], 0.0, 256.0, OP.is_ge, OP.mult)
+    vset(T.kc[:, 8:16], 256.0 * (127 + CAPP))
     c_m = tt(T.t1[:, 32:544:4], T.tm[:, 0:128], T.tm[:, 128:256], OP.add, h)
-    ts(T.pb[:, 6:7], T.pb[:, 1:2], 31, None, OP.bitwise_and, None)
-    h = ts(T.pb[:, 7:8], T.pb[:, 1:2], 1, None, OP.bitwise_and, None)
-    for b in range(2):
-        h2 = vset(T.c3[:, 264 * b:264 * b + 8], BIG, c_c3)
-    c_pb = vcopy(T.pbh[:, 0:8], T.pb[:], h)
     for k in (0, 3, 5):
         c_tx2 = act(T.tx[:, k:32:8], T.i8[:, 0:4], i_8, c_tx)
     act(T.m2[:, 0:256:2], T.t1[:, 32:544:4], c_m)
     c_m2 = lin(T.m2[:, 1:256:2], T.t1[:, 32:544:4], -1.0, 0.0)
     for k in (0, 3):
         c_t22 = act(T.t2x[:, k:32:4], T.pt[:], i_t, c_t2)
-    for k in (2, 5, 268):
-        c_s3 = lin(T.c3[:, k:k + 1], T.i8[:, 0:1], 0.0, 0.0, h2)
+    c_f = lin(T.pf[:, 3:4], T.pf[:, 1:2], 1 / 128, 0.0, i_f)
     col = [T.pbh[:, i:i + 1] for i in range(10)]
     rho = col[5]
 
     xq = do("v", lambda: V.quantize_mx(T.xq[:], T.xs[:], T.xh[:]), ldx, ldp, c_x)
     z = mm(T.z, 134, T.xq, T.xs, AT, 0, xq)
-    c_dm = ts(T.dm[:], T.dd[:], 0.0, 0.9375, OP.is_equal, OP.mult)
-    for b in range(2):
-        c_c3 = ts(T.c3[:, 264 * b + 8:264 * b + 264:2], T.dd[:], 0.0, BIG, OP.is_lt, OP.mult)
+    for k, c in enumerate((240, 15, 31)):
+        h = ts(T.pb[:, 2 + 2 * k:4 + 2 * k], T.pb[:, 0:2], c, None, OP.bitwise_and, None, i_p)
+    ts(T.dz[:], T.dd[:], 0.0, BIG, OP.not_equal, OP.mult)
+    c_pb = vcopy(T.pbh[:, 0:8], T.pb[:], h)
     b0, b1, b2 = [T.bt[:, i:i + 1] for i in range(3)]
     h0 = ts(T.bt[:, 0:2], T.z[:, 2:4], 0.0, None, OP.is_lt, None, z)
     h1 = ts(b2, T.z[:, 4:5], 0.0, 2.0, OP.is_lt, OP.mult)
@@ -276,74 +265,95 @@ def rank_program(g, core, T, topo):
     hb = ts(T.bk[:, 0:1], b1, b2, 2.0, OP.add, OP.mult)
     cn = count("1", T.t1, 8, T.cn, h)
     h = ts(T.bk[:, 1:2], T.bk[:, 0:1], b0, None, OP.add, None, hb)
-    hz = tt(T.pd[:, 0:128], T.z[:, AT:AT + 128], T.dm[:], OP.mult)
+    tt(T.pd[:, 0:128], T.z[:, AT:AT + 128], T.dz[:], OP.is_gt)
+    hb = ts(T.sg[:, 1:2], T.bk[:, 1:2], 2.0 * CAPP, T.pf[:, 3:4], OP.mult, OP.add, h, c_f)
+    hz = lin(T.junk[:, 0:128], T.pd[:, 0:128], T.pf[:, 0:1], T.sg[:, 1:2], hb, sum_to=T.sg[:, 0:1])
     for k in range(2):
-        ts(T.t2[:, k:64:2], T.t2x[:], T.bk[:, 1:2], col[2 + 2 * k], OP.is_equal, OP.mult, h, c_t22)
-    hb = lin(T.sg[:, 1:2], T.bk[:, 1:2], 256.0 * CAPP, T.pf[:, 1:2], h, i_f)
-    hz = total(T.sg[:, 0:1], T.junk[:, 0:128], T.pd[:, 0:128], FN.Sign, hz)
-    h = red(T.key[:, 0:1], T.cn[:, 0:8], OP.max, cn)
+        ts(T.t2[:, k:64:2], T.t2x[:], T.bk[:, 1:2], col[2 + 2 * k], OP.is_equal, OP.mult, c_t22)
+    hv = scan(T.kc[:, 0:8], T.cn[:, 0:8], T.kc[:, 8:16], cn, ops=(OP.max, OP.min))
+    h = red(T.key[:, 0:1], T.cn[:, 0:8], OP.max)
+    ms = ts(T.ms[:, 0:1], T.kc[:, 7:8], T.sg[:, 0:1], None, OP.add, None, hv, hz)
+    note_out(T.ms[:, 0:1], "rm1", "rn1", ms, i_v)
+    send([xfer(T.ms[:, 0:1], [T.nlx[:, 4 + ap:5 + ap]], [T.cores[far[0]]], MSG["far"], "n1x"),
+          xfer(T.ms[:, 0:1], [T.nl1[:, 8 * ap:8 * ap + 1]], [T.cores[peer[0]]], MSG["peer"], "n1")])
     for k in range(2):
         h2 = ts(T.t2[:, 64 + k:576:2], T.r2[:], T.key[:, 0:1], None, OP.is_equal, None, h, i_r)
-    hb = lin(T.sg[:, 2:3], T.sg[:, 0:1], T.pf[:, 0:1], T.sg[:, 1:2], hb, hz)
-    hv = lin(T.vv[:, 0:1], T.key[:, 0:1], -1.0, T.pf[:, 3:4], h, fn=FN.Relu)
-    ms = ts(T.ms[:, 0:1], T.vv[:, 0:1], -256.0, T.sg[:, 2:3], OP.mult, OP.add, hv)
-    send([xfer(T.ms[:, 0:1], T.rm1[:], relays, MSG["relay"], "rn1")], ms, i_c)
-    note_same(T.ms[:, 0:1], "nl1", "n1")
     lp = count("2", T.t2, 16, T.lp, h2)
     ts(T.tri[:, 0:128], T.dd[:, 127::-1], 0.0, BIG, OP.is_lt, OP.mult)
-    c_tri = vset(T.tri[:, 128:256], BIG)
+    ts(T.dm[:], T.dd[:], 0.0, 0.9375, OP.is_equal, OP.mult)
     XQ, L1 = ("xq", "xs"), ("land1c", "land1s")
     o1 = vcopy(T.off1[:], T.lp[:, 0:16], lp)
     pk = [pick("slot1", XQ, 134, 128 * e, 128 * e + 128, T.off1[:, 8 * e:8 * e + 8], o1) for e in range(2)]
-    send_cross("1", *pk[0])
+    send_four("slot1c", "r1c", "rc1", pk[0][0])
+    send_four("slot1s", "r1s", "rs1", pk[0][1])
     send_same("slot1c", "land1c", "a1", pk[1][0])
     send_same("slot1s", "land1s", "a1", pk[1][1])
+    i_1 = iota(T.r1[:], [[0, 8], [1, 16]], 0)
+    if me == 0:
+        i_1 = iota(T.nk[:, 0:32], [[128, 8], [0, 4]], 8192 - 128)
+    a1, n1x = ("a1", 2 * ncol), ("n1x", 48 if ap == 0 else 16)
+    if ap == 0:
+        send([xfer(T.nlx[:], [T.nlx[:]], [T.cores[peer[0]]], (0, 16), "n1x")], n1x)
     i = pos.index(me)
     own1 = pick("land1", XQ, 134, 32 * me, 32 * me + 32, T.off1[:, 2 * i:2 * i + 2], o1)
 
     load("y", "ldz", T.land3c[:, 256:258].bitcast(dt.uint8), T.xq[:, 0:2].bitcast(dt.uint8), xq)
     ldz = load("y", "ldz", T.land3s[:, 256:258], T.xs[:, 0:2], xq)
-    own_n = vcopy(T.nl1[:, 8 * me:8 * me + 1], T.ms[:, 0:1], ms)
-    c_rep = vcopy(T.rep[:], T.rf[:], i_c)
-    vset(T.t3[:], 0.0)
-    h5 = lin(T.rb[:], T.r2[:], 0.0, 0.0, i_r)
-    lin(T.pf[:, 2:3], col[6], -256.0, -256.0 * CAPP * me - 128.0, c_pb)
-    lin(T.nb[:], T.r2[:], 0.0, 0.0)
-    lin(T.rb[:, 0:256:32], T.i8[:], 0.0, BIG, h5)
-    lin(T.nf[:], T.r2[:], 0.0, 0.0)
+    own_n = vcopy(T.nl1[:, 8 * ap:8 * ap + 1], T.ms[:, 0:1], ms)
     for k in range(2):
         for j in range(2):
-            h = lin(T.kv[:, 16 * j + k:16 * j + 16:2], T.pt[:], 2.0, 4096.0 + k)
-    if me == 0:
-        vset(T.wa[:], 0.0)
+            lin(T.kv[:, 16 * j + k:16 * j + 16:2], T.pt[:], 0.125, 256.0 + k / 16)
     for a in range(4):
-        for k in range(4):
-            h2 = vset(quad("kv", a, slice(32 + k, 64, 4)), 4096.0 + 2 * pos[4 * (k // 2) + a] + k % 2)
-    lin(T.one[:], T.i8[:], 0.0, 1.0)
-    h3 = lin(T.rst9[:], T.r2[:, 0:72], 0.0, 1.0)
-    lin(col[8], col[3], 1.0, 128.0)
-    h4 = lin(T.k8[:], rho, 16.0, 2.0 * me)
-    lin(T.nft[:, 256:264], T.i8[:], 0.0, -1.0)
-    lin(T.rst9[:, 0:72:9], T.i8[:], 0.0, 0.0, h3)
-    lin(T.gg[:], T.i8[:], 256.0, T.k8[:, 0:1], h4)
-    c_s = lin(T.it[:, 0:72:9], T.i8[:], 256.0, T.k8[:, 0:1])
-    c_w = do("v", lambda: V.quantize_mx(T.wq[:], T.ws[:], T.wh[:]), ldw)
-    h = turn(T.kt[:], T.kv[:], h, h2)
-    vcopy(T.kk[:, 0:2], T.kt[:, 0:64:32], h)
-    c_k = ts(T.kk[:, 2:4], T.kt[:, 0:64:32], -7.5, None, OP.add, None)
-
-    a1, n1 = ("a1", 2 * ncol), ("n1", nmsg)
-    h = vcopy(T.nlf[:], T.nl1[:, 0:64:8], n1, own_n)
-    rp = act(T.rp[:], T.nlf[:].indirect(T.rep[:]), h, c_rep)
+        hk = lin(quad("kv", a, slice(32, 64)), quad("kq", a, slice(0, 32)), 1 / 16, 256.0 + pos[a] / 8, i_v)
     if me == 0:
-        h = ts(T.wa[:, 0:8], T.nlf[:], -1.0, 256.0, OP.mult, OP.add, h)
+        c_wa = vset(T.wa[:], 0.0)
+    h = vset(T.c3[:], 0.0)
+    vset(T.t3[:], 0.0)
+    for b in range(2):
+        h3 = vset(T.c3[:, 264 * b:264 * b + 8], BIG, h)
+        ts(T.c3[:, 264 * b + 8:264 * b + 264:2], T.dd[:], 0.0, BIG, OP.is_lt, OP.mult)
+    h = turn(T.kt[:], T.kv[:], hk)
+    if me:
+        vset(T.cl[:, 8 * me:8 * me + 1], -WHOLE)
+        vset(T.cl[:, 8 * me + 8:8 * me + 9], WHOLE)
+    vcopy(T.kk[:, 0:2], T.kt[:, 0:64:32], h)
+    c_k = ts(T.kk[:, 2:4], T.kt[:, 0:64:32], -7.5 / 16, None, OP.add, None)
+    for j in range(0, N, 2):
+        i_c = lin(T.rf[:, 2 * came[j]:2 * came[j] + 4], T.v16[:, 0:4], 1 / 128, float(j))
+    h5 = lin(T.rb[:], T.r2[:], 0.0, 0.0, i_r)
+    lin(T.pf[:, 2:3], col[7], -256.0, -256.0 * CAPP * me - 128.0, c_pb)
+    h6 = lin(T.nb[:], T.r2[:], 0.0, 0.0)
+    lin(T.rb[:, 0:256:32], T.i8[:], 0.0, BIG, h5)
+    lin(T.one[:], T.r2[:, 0:16], 0.0, 1.0)
+    h5 = lin(T.rst9[:], T.r2[:, 0:72], 0.0, 1.0)
+    lin(T.nb[:, 1:256:32], T.i8[:], 128.0, 0.0, h6)
+    lin(col[8], col[3], 1.0, 128.0)
+    h4 = lin(T.pf[:, 4:5], rho, 1.0, me / 8)
+    lin(T.nft[:, 256:264], T.i8[:], 0.0, -1.0)
+    lin(T.rst9[:, 0:72:9], T.i8[:], 0.0, 0.0, h5)
+    lin(T.gg[:], T.i8[:], 16.0, T.pf[:, 4:5], h4)
+    c_s = lin(T.it[:, 0:72:9], T.i8[:], 16.0, T.pf[:, 4:5])
+
+    vcopy(T.nlf[:, 6:8], T.nl1[:, 0:16:8], ("n1", 8), own_n)
+    if me == 0:
+        ts(T.wa[:, 0:2], T.nl1[:, 0:16:8], 256.0, -1.0, OP.min, OP.mult, c_wa)
+        for j in (4, 0, 2):
+            h = ts(T.wa[:, came[j]:came[j] + 2], T.nlx[:, j:j + 2], 256.0, -1.0, OP.min, OP.mult, n1x)
+    c_w = do("v", lambda: V.quantize_mx(T.wq[:], T.ws[:], T.wh[:]), ldw, i_1)
+    if me == 0:
         h = turn(T.wb[:, 0:32], T.wa[:, 0:32], h)
-        h = red(T.wa[:, 32:33], T.wb[:, 0:32], OP.max, h)
+        h = lin(T.junk[:, 0:32], T.wb[:, 0:32], 1.0, 0.0, h, sum_to=T.wa[:, 32:33])
+    c_tri = vset(T.tri[:, 128:256], BIG)
+    c_rep = vcopy(T.rep[:], T.rf[:], i_c)
+    for k in (2, 5, 268):
+        vset(T.c3[:, k:k + 1], 0.0, h3)
+    if ap == 0:
+        hn = vcopy(T.nlf[:, 0:6], T.nlx[:], n1x)
+    if me == 0:
         h = turn(T.wb[:, 32:64], T.wa[:, 32:64], h)
         for a in range(4):
-            w4 = cast(T.wc[:, 8 * a:8 * a + 8], T.wb[32 * a:32 * a + 1, 32:40], h)
-    h = turn(T.rt[:], T.rp[:], rp)
-    ab = lin(T.ab[:], T.rt[:], 1.0, T.pf[:, 2:3], h, c_s, fn=FN.Abs)
+            h2 = act(T.wa[0:1, 64 + a:96:4], T.wb[32 * a:32 * a + 1, 32:40], h)
+        w4 = do("p", lambda: g.partition_broadcast(T.wc[:], T.wa[0:1, 64:96], 128), h2, i_1)
 
     gs = [T.ga, T.gb]
     wd = [(slice(128 * b, 128 * b + 128), slice(128 * b, 128 + 256 * b), 128 + 128 * b) for b in range(2)]
@@ -352,107 +362,134 @@ def rank_program(g, core, T, topo):
     for b in range(2):
         w, w2, n = wd[b]
         h = tt(T.pd[:, w], gs[b][:, w], T.dm[:], OP.mult, gm[b], hz)
-        th.append(total(T.thr[:, b:b + 1], T.junk[:, w], T.pd[:, w], COPY, h))
+        th.append(lin(T.junk[:, w], T.pd[:, w], 1.0, 0.0, h, sum_to=T.thr[:, b:b + 1]))
         mx.append(scan(T.xg[:, w2], gs[b][:, n - 1::-1], T.tri[:, 0:n], c_tri, ops=(OP.max, OP.min)))
+        if ap and b == 0:
+            hn = vcopy(T.nlf[:, 0:6], T.nlx[:], n1x)
     for b in range(2):
         at = 128 * b + wd[b][2] - 1
-        if me == 0 and b:
-            w4 = tt(T.wc[:, 32:48], T.wc[:, 0:16], T.wc[:, 16:32], OP.max, w4)
-        t3 = ts(T.t3[:, b:512:4], T.c3[:, 528:656], T.xg[:, at:at + 1], T.thr[:, b:b + 1], OP.add, OP.is_lt, mx[b], th[b], c_c3)
-    if me == 0:
-        w4 = tt(T.wc[:, 48:56], T.wc[:, 32:40], T.wc[:, 40:48], OP.max, w4)
+        t3 = ts(T.t3[:, b:512:4], T.c3[:, 528:656], T.xg[:, at:at + 1], T.thr[:, b:b + 1], OP.add, OP.is_lt, mx[b], th[b])
+    rp = act(T.rp[:], T.nlf[:].indirect(T.rep[:]), hn, c_rep)
     sp = count("3", T.t3, 0, T.sp, t3)
-    size = T.cl[:, 8 * me:8 * me + 1]
-    if me == 0:
-        ts(T.en[:, 0:8], T.wc[:, 48:56], 0.0, None, OP.is_le, None, w4)
-        h = ts(T.en[:, 8:16], T.wc[:, 48:56], 128.0, None, OP.is_gt, None)
-    for b in range(2):
-        t5 = ts(T.t5[:, b:528:2], T.c3[:, 264 * b:264 * b + 264], 0.5, T.t3[:, b:b + 1], OP.is_lt, OP.mult, c_s3)
-        if me == 0 and b == 0:
-            he = scan(T.en[:, 16:24], T.en[:, 7::-1], T.en[:, 15:7:-1], h)
-    if me == 0:
-        sz = ts(size, T.sp[:, 0:1], T.en[:, 23:24], 2.0, OP.add, OP.mult, sp, he)
-    else:
-        sz = ts(size, T.sp[:, 0:1], 2.0, None, OP.mult, None, sp)
+    size, e8 = T.szb[:, 0:1], T.en[:, 96:97]
 
-    note_out(size, "rm2", "rn2", sz)
+    def half(k):
+        w = slice(128 * k, 128 * k + 128)
+        return lin(T.ab[:, w], T.rt[:, w], 1.0, T.pf[:, 2:3], turn(T.rt[:, w], T.rp[:, w], rp), c_s, fn=FN.Abs)
+
+    if me == 0:
+        ts(T.en[:, 0:32], T.wc[:], -8192.0, None, OP.is_le, None, w4)
+        h = ts(T.en[:, 32:64], T.wc[:], 128.0 - 8192, None, OP.is_gt, None)
+    for b in range(2):
+        t5 = ts(T.t5[:, b:528:2], T.c3[:, 264 * b:264 * b + 264], 0.5, T.t3[:, b:b + 1], OP.is_lt, OP.mult)
+        if me == 0 and b == 0:
+            he = scan(T.en[:, 64:96], T.en[:, 31::-1], T.en[:, 63:31:-1], h)
+    if me == 0:
+        sz = ts(size, T.sp[:, 0:1], T.en[:, 95:96], 0.125, OP.add, OP.mult, sp, he)
+    ab = [half(0)]
+    if me:
+        sz = ts(size, T.sp[:, 0:1], 0.125, None, OP.mult, None, sp)
+
+    send([xfer(size, [T.rm2[:]], [k], HAND[j], "rn2") for j, k in enumerate(relays)], sz)
     note_same(size, "cl", "c2")
     cu = count("5", T.t5, 4, T.cn, t5)
+    ab.append(half(1))
     qd = ts(T.qd[:], T.t3[:, 0:2], -257.0, 256.0, OP.mult, OP.add)
-    sm = scan(T.sm[:], T.rb[:], T.ab[:], ab, ops=(OP.add, OP.min))
+    scan(T.sm[:, 0:128], T.rb[:, 0:128], T.ab[:, 0:128], ab[0], ops=(OP.add, OP.min))
     h = tt(T.ti[:], T.cn[:, 1:3], T.qd[:], OP.add, qd, cu)
-    hq = [(vcopy if a % 2 else act)(T.mq[0:32, a:32:4], quad("sm", a, slice(31, 256, 32)), sm) for a in range(4)]
+    sm = scan(T.sm[:, 128:256], T.rb[:, 0:128], T.ab[:, 128:256], ab[1], ops=(OP.add, OP.min))
+    hq = [act(T.mq[0:32, a:32:4], quad("sm", a, slice(31, 256, 32)), sm) for a in range(4)]
     ts(T.uv[:, 0:2], T.ti[:], 3, 15, OP.logical_shift_right, OP.bitwise_and, h)
     h = ts(T.uv[:, 2:4], T.ti[:], 256 + 128 + 7, None, OP.bitwise_and, None)
     if me == 0:
-        he = ts(T.e2[:], T.en[:, 23:24], 2.0, None, OP.mult, None)
-    hm = scan(T.mr[0:32, :], T.rb[0:32, 0:256:8], T.mq[0:32, :], *hq, ops=(OP.add, OP.min))
+        he = ts(e8, T.en[:, 95:96], 0.125, None, OP.mult, None)
     h = vcopy(T.uvf[:], T.uv[:], h)
-    hm = tt(T.nb[0:32, 0:256:32], T.mr[0:32, 3:32:4], T.c128[0:32, :], OP.add, hm)
-    for a in range(1, 4):
-        nb = act(quad("nb", a, slice(0, 256, 32)), T.nb[0:32, 0:256:32], hm)
     for b in range(2):
         ts(T.t4[:, b:64:2], T.v16[:], T.uvf[:, 2 + b:3 + b], None, OP.is_equal, None, h)
         for k in range(2):
             h2 = ts(T.t4[:, 64 + b + 2 * k:576:4], T.r1[:], T.uvf[:, b:b + 1], rho if k else col[8 if b else 3], OP.is_equal, OP.mult)
+    hm = scan(T.mr[0:32, :], T.rb[0:32, 0:256:8], T.mq[0:32, :], *hq, ops=(OP.add, OP.min))
     pp = count("4", T.t4, 16, T.pp, h2)
-    nw = turn(T.nw[:], T.nb[:], nb)
+    for a in range(4):
+        nb = act(quad("nb", a, slice(0, 256, 32)), T.mr[0:32, 3:32:4], hm)
     plw = act(T.plw[:], T.pp[:, 0:16], pp)
 
     c2 = ("c2", nmsg)
     if me:
-        he = end = scan(T.end[:], T.one[:], T.cl[:, 0:64:8], c2, sz)
-    before = T.end[:, me - 1:me] if me else T.e2[:, 0:1]
-    ts(T.vi[:], T.kk[:, 2:4], before, 0.0625, OP.subtract, OP.mult, he, c_k)
-    h = ts(T.vx[:], T.kk[:, 0:2], before, None, OP.subtract, None)
-    if me:
-        hd = ts(T.d256[:], T.cl[:, 0:64:8], -1.0, 512.0, OP.mult, OP.add)
-    ov = [ts(T.ov[:, 2 * k:2 * k + 1], T.vi[:, k:k + 1], -16.0, T.vx[:, k:k + 1], OP.mult, OP.add, h) for k in range(2)]
+        ov = []
+        for k in range(2):
+            for j, n in ((1, me + 2), (0, me)):
+                h = scan(T.sq[:, 32 * k + 16 * j:32 * k + 16 * j + n], T.one[:, 0:n], T.cl[:, 0:8 * n:8], c2, c_k,
+                         ops=(OP.mult, OP.subtract), init=T.kk[:, 2 * j + k:2 * j + k + 1])
+            ov.append(h)
+        done = h
+        for k in range(2):
+            ov[k] = ts(T.ov[:, 2 * k:2 * k + 1], T.sq[:, 32 * k + me - 1:32 * k + me], T.sq[:, 32 * k + me + 17:32 * k + me + 18], 16.0,
+                       OP.subtract, OP.mult, ov[k])
+            if k == 0:
+                nj = turn(T.nj[:], T.nb[:], nb)
+    else:
+        ts(T.vi[:], T.kk[:, 2:4], e8, None, OP.subtract, None, he, c_k)
+        done = h = ts(T.vx[:, 0:2], T.kk[:, 0:2], e8, None, OP.subtract, None)
+        nj = turn(T.nj[:], T.nb[:], nb)
+        ov = [ts(T.ov[:, 2 * k:2 * k + 1], T.vi[:, k:k + 1], T.vx[:, k:k + 1], -16.0, OP.subtract, OP.mult, h) for k in range(2)]
     o3 = vcopy(T.off3[:], T.plw[:].indirect(T.ov[:, 0:1]), ov[0], plw)
     on = vcopy(T.offn[:], T.plw[:].indirect(T.ov[:, 2:3]), ov[1])
-    send_cross("3", *pick("slot3", L1, 256, 0, 128, T.off3[:, 0:8], o3, a1, *own1))
-    n3 = act(T.n3[:], T.nw[:].indirect(T.offn[:, 0:4]), on, nw)
+    lin(T.cl[:, 8 * me:8 * me + 1], size, 0.0, 0.0, done)
+    own_c = act(T.cl[:, 8 * me + 8:8 * me + 9], size)
+    n3 = act(T.n3[:], T.nj[:].indirect(T.offn[:, 0:4]), on, nj)
+    pc, ps = pick("slot3", L1, 256, 0, 128, T.off3[:, 0:8], o3, a1, *own1)
+    send_two("slot3c", "r3c", "rc3", pc)
+    send_four("slot3s", "r3s", "rs3", ps)
     pc, ps = pick("slot3", L1, 256, 128, 256, T.off3[:, 8:16], o3)
     h = turn(T.nt3[:], T.n3[:], n3)
     hc = pickc(T.land3c[:, 32 * me:32 * me + 32], T.land1c[:], T.off3[:, 2 * i:2 * i + 2])
-    m3 = vcopy(T.m3[:], T.nt3[:, 0:64:32], h)
+    if me:
+        end = scan(T.end[:], T.one[:, 0:9], T.cl[:, 0:72:8], own_c)
+    m3 = [ts(T.m3[:, k:k + 1], T.nt3[:, 32 * k:32 * k + 1], T.nt3[:, 32 * k + 1:32 * k + 2], None, OP.add, None, h) for k in range(2)]
     own3 = (hc, act(T.land3s[:, 32 * me:32 * me + 32], T.land1s[:].indirect(T.off3[:, 2 * i:2 * i + 2])))
-    note_out(T.m3[:, 0:1], "rm3", "rn3", m3)
+    note_out(T.m3[:, 0:1], "rm3", "rn3", m3[0])
     send_same("slot3c", "land3c", "a3", pc)
     send_same("slot3s", "land3s", "a3", ps)
-    note_same(T.m3[:, 1:2], "nl3", "n3")
-    own_n3 = vcopy(T.nl3[:, 8 * me:8 * me + 1], T.nt3[:, 32:33])
+    note_same(T.m3[:, 1:2], "nl3", "n3", m3[1])
+    c_nf = lin(T.nf[:], T.r2[:], 0.0, 0.0)
 
+    hd = ts(T.d256[:], T.cl[:, 0:72:8], -1.0, 32.0, OP.mult, OP.add, c2, own_c)
     if me == 0:
-        ts(T.it[:, 0:72:9], T.gg[:], T.e2[:, 0:1], None, OP.subtract, None)
-        h = tt(T.nk[:, 0:8], T.nw[:, 0:256:32], T.en[:, 8:16], OP.mult, nw)
-        end = scan(T.end[:], T.one[:], T.cl[:, 0:64:8], c2)
-        hd = ts(T.d256[:], T.cl[:, 0:64:8], -1.0, 512.0, OP.mult, OP.add)
-        nk = scan(T.nk[:, 8:16], T.en[:, 7::-1], T.nk[:, 7::-1], h)
-        hd = ts(T.d256[:, 0:1], T.d256[:, 0:1], T.e2[:, 0:1], None, OP.add, None, hd)
-    for d in range(N):
-        h2 = ts(T.it[:, 1 + d:72:9], T.gg[:], T.end[:, d:d + 1], T.d256[:, d:d + 1], OP.is_ge, OP.mult, hd, end)
+        end = scan(T.end[:], T.one[:, 0:9], T.cl[:, 0:72:8])
+        ts(T.it[:, 0:72:9], T.gg[:], e8, None, OP.subtract, None)
+    own_n3 = ts(T.nl3[:, 8 * me:8 * me + 1], T.nt3[:, 32:33], T.nt3[:, 33:34], None, OP.add, None)
+    if me == 0:
+        hd = ts(T.d256[:, 1:2], T.d256[:, 1:2], e8, None, OP.add, None, hd)
+    for d in range(N)[::-1]:
+        k = d + (d >= me)
+        h2 = ts(T.it[:, 1 + d:72:9], T.gg[:], T.end[:, k:k + 1], T.d256[:, k:k + 1], OP.is_ge, OP.mult, end, *([hd] if me or d == 0 else []))
+    if me == 0:
+        nk = tt(T.nk[:, 32:64], T.wc[:], T.nk[:, 0:32], OP.add)
+        ts(T.vx[:, 2:3], T.gg[:, 0:1], e8, 258.0, OP.is_lt, OP.mult)
     h = scan(T.its[:], T.rst9[:], T.it[:], h2)
     if me == 0:
-        ts(T.nft[:, 257:258], T.nk[:, 15:16], -1.0, None, OP.add, None, nk)
-    h = vcopy(T.xi[:], T.its[:, 8:72:9], h)
-    h = ts(T.xsh[:], T.xi[:], 4, None, OP.logical_shift_right, None, h)
-    oz = ts(T.offz[:], T.xsh[:], 256.0, None, OP.min, None, h)
+        nk = tt(T.nk[:, 64:96], T.nk[:, 32:64], T.en[:, 32:64], OP.mult, nk)
+    h = ts(T.xsh[:], T.its[:, 8:72:9], -0.4375, None, OP.add, None, h)
     if me == 0:
-        h = ts(T.nk[:, 16:17], T.xsh[:, 0:1], 1.0e6, None, OP.is_gt, None)
-        oz = ts(T.offz[:, 0:1], T.xsh[:, 0:1], 256.0, T.nk[:, 16:17], OP.min, OP.add, h)
+        nk = scan(T.nk[:, 96:128], T.en[:, 31::-1], T.nk[:, 95:63:-1], nk)
+        ts(T.offz[:, 1:8], T.xsh[:, 1:8], 256.0, None, OP.min, None, h)
+        oz = ts(T.offz[:, 0:1], T.xsh[:, 0:1], 256.0, T.vx[:, 2:3], OP.min, OP.add)
+        ts(T.nft[:, 257:258], T.nk[:, 127:128], -1.0, None, OP.add, None, nk)
+    else:
+        oz = ts(T.offz[:], T.xsh[:], 256.0, None, OP.min, None, h)
 
     a3 = ("a3", 2 * ncol)
     fc = pickc(T.fq[:], T.land3c[:], T.offz[:], a3, ldz, oz, *own3)
     fs = act(T.fs[:], T.land3s[:].indirect(T.offz[:]), a3, ldz, oz, *own3)
     yp = do("t", lambda: E.matmul_mx(T.yp[:, 0:128], T.wq[:], T.ws[:], T.fq[:], T.fs[:], True, True), fc, fs, c_w)
     load("y", "dout", T.oc[:], T.fq[:].bitcast(dt.uint8), fc)
-    h = vcopy(T.nf[:, 0:256:32], T.nl3[:, 0:64:8], ("n3", nmsg), own_n3)
+    h = vcopy(T.nf[:, 0:256:32], T.nl3[:, 0:64:8], ("n3", nmsg), own_n3, c_nf)
     h = turn(T.nft[:, 0:256], T.nf[:], h)
     for k in range(4):
         load("y", "dout", T.osc[4 * k:4 * k + 4, :], T.fs[32 * k:32 * k + 4, :], fs)
     ys = act(T.ysb[:], T.yp[:, 0:128], yp)
-    load("s", "dout", T.y[:], T.ysb[:], ys)
-    no = vcopy(T.no[:], T.nft[:].indirect(T.offz[:]), h)
-    load("y", "dout", T.num[:], T.no[32 * am:32 * am + 1, :], no)
+    load("y", "dout", T.y[:], T.ysb[:], ys)
+    no = vcopy(T.no[:, 0:64], T.nft[:].indirect(T.offz[:, 0:4]), h), act(T.no[:, 64:128], T.nft[:].indirect(T.offz[:, 4:8]), h)
+    load("y", "dout", T.num[:], T.no[32 * am:32 * am + 1, :], *no)
     wait("p", [(s, cnt[s]) for s in ("qv", "qs", "qt", "qp", "dout", "ls", "ldz", "ldp", "ldx", "ldw")])

from concourse.bass import DstId, RemoteDMATransfer
from concourse.mybir import dt, AluOpType, AxisListType, ActivationFunctionType

OP = AluOpType
FN = ActivationFunctionType
COPY = FN.Copy
X = AxisListType.X
N, P, L, CAPP = 8, 128, 3, 32
BIG = 1.0e29
WHOLE = 1.5 * 2 ** 23
AT = 6

SCRATCH = {}
for _kind, _list in {
    "bfloat16": "xh 536 wh 512 dd 128 tm 256 m2 256 tx 32 t2x 32 r2 256 r1 128 t1 544 t2 576 t3 512 t5 528 t4 576 c3 656 "
                "one 16 cl 72 rm2 1 pbh 10 bt 4 bk 2 key 2 uvf 4 v16 32 szb 2 nb 256 nj 256",
    "float8_e4m3fn_x4": "xq 134 wq 128 q1 136 q2 144 q3 128 q5 132 q4 144 slot1c 256 land1c 256 slot3c 256 land3c 258 fq 128 r1c 64 r3c 64",
    "uint8": "xs 134 ws 128 s1 136 s2 144 s3 128 s5 132 s4 144 slot1s 256 land1s 256 slot3s 256 land3s 258 fs 128 r1s 64 r3s 64",
    "uint16": "rep 16 ms 2 nl1 16 nlx 6 rm1 1 off1 16 ov 4 off3 16 offn 16 nl3 64 m3 2 offz 8 rm3 1",
    "int32": "pb 8 ti 2 uv 4 vi 2 xsh 8",
    "float32": "i8 8 pt 8 rst9 72 kc 16 dz 128 sq 64 gg 8 dm 128 tri 256 kv 64 kt 64 kk 4 kq 32 vx 4 pd 256 thr 2 xg 384 "
               "qd 2 plw 16 n3 64 nt3 64 end 9 d256 9 it 72 its 72 nf 256 nft 264 no 128 ysb 128 "
               "en 97 nk 128 junk 256 pf 5 sg 2 nlf 8 rp 256 rt 256 ab 256 rb 256 sm 256 mq 32 mr 32 wa 96 wb 64 wc 32 rf 16",
}.items():
    _w = _list.split()
    for _i in range(0, len(_w), 2):
        SCRATCH[_w[_i]] = ("sbuf", [128, int(_w[_i + 1])], _kind)
for _n in ("z", "cn", "lp", "ga", "gb", "sp", "pp", "yp"):
    SCRATCH[_n] = ("psum", [128, 512], "float32")
SEMAPHORES = ["qv", "qs", "qt", "qp", "ldp", "ldx", "ldw", "ldz", "dout", "ls",
              "a1", "n1", "n1x", "c2", "a3", "n3", "rc1", "rs1", "rn1", "rn2", "rc3", "rs3", "rn3"]


def wiring(T, topo):
    cores = T.cores
    same = [[r for r in range(N) if cores[r] in topo.cores_of(cores[s]) or topo.same_plane(cores[s], cores[r])] for s in range(N)]
    cross = [[r for r in range(N) if r not in same[s]] for s in range(N)]
    relays = [[k for k in topo.cores_of(c) if k not in cores and topo.die(k) == topo.die(c)
               and all(topo.may_write(k, cores[r]) for r in cross[s])][:2] for s, c in enumerate(cores)]
    pair = [[r for r in range(N) if cores[r] in topo.cores_of(c)] for c in cores]
    assert all(len(p) == 2 and p[1] == p[0] + 1 for p in pair)
    return same, cross, relays, pair


def eng(topo, src, dst, a, b):
    return sum(1 << e for e in topo.engines(src, dst)[a:b])


def dest(topo, src, dst):
    rid, pid = topo.addr(dst, src)
    return DstId(rid=rid, pnc=pid)


HAND = ((0, 8), (8, 16))
COL = {"peer": (8, 16), 0: (0, 4), 1: (4, 8)}
MSG = {"relay": (8, 16), "far": (0, 8), "peer": (8, 16)}


def view(T, buf, a, b):
    v = T[buf][:, a:b]
    return v.bitcast(dt.uint8) if buf[-1] == "c" else v


def seat(T, land, s, r):
    at = 8 * (s + (land == "cl" and s > r))
    return T[land][:, at:at + 1]


def relay_program(g, core, T, topo, s, group, first, one, at):
    to = [T.cores[r] for r in group]
    sent = [0]

    def go(sem, tr):
        g.wait_ge(T.sem[sem], 8)
        g.remote_dma_fused(tr, local_sem=T.sem.ls)
        sent[0] += 8

    def write(d, a, b, rsem, src, dst):
        return RemoteDMATransfer(dst_ids=[dest(topo, core, d)], dma_engine_mask=eng(topo, core, d, a, b), remote_sem=T.sem[rsem], src=src, dst=dst)

    def both(sem, buf, land, rsem):
        go(sem, [write(T.cores[one], 0, 8, rsem, view(T, buf, 0, 64), view(T, land, 32 * first, 32 * first + 64))])

    def note(sem, src, land, rsem):
        go(sem, [RemoteDMATransfer(dst_ids=[dest(topo, core, d) for d in to], dma_engine_mask=eng(topo, core, to[0], 0, 8), remote_sem=T.sem[rsem],
                                   srcs=[T[src][:]], dsts=[seat(T, land, s, r) for r in group])])

    go("rn1", [write(to[0], 0, 8, "n1x", T.rm1[:], T.nlx[:, at:at + 1])])
    both("rc1", "r1c", "land1c", "a1")
    both("rs1", "r1s", "land1s", "a1")
    note("rn2", "rm2", "cl", "c2")
    go("rc3", [write(d, 4 * i, 4 * i + 4, "a3", view(T, "r3c", 32 * i, 32 * i + 32), view(T, "land3c", 32 * s, 32 * s + 32)) for i, d in enumerate(to)])
    both("rs3", "r3s", "land3s", "a3")
    note("rn3", "rm3", "nl3", "n3")
    g.wait_ge(T.sem.ls, sent[0])


def rank_program(g, core, T, topo):
    same_all, cross_all, relays_all, pair_all = wiring(T, topo)
    me = T.rank_of(core)
    if me is None:
        for s in range(N):
            if core in relays_all[s]:
                i = relays_all[s].index(core)
                relay_program(g, core, T, topo, s, cross_all[s][2 * i:2 * i + 2], pair_all[s][0], cross_all[s][2 * i + pair_all[s].index(s)],
                              same_all[s].index(s))
        return
    same, cross, relays, pair = same_all[me], cross_all[me], relays_all[me], pair_all[me]
    pos = cross + same
    assert pos == [pos[0] + sum((pos[k] - pos[0]) * (i // k % 2) for k in (4, 2, 1)) for i in range(N)]
    am, ap = same.index(me), pair.index(me)
    peer = [r for r in pair if r != me]
    far = [r for r in same if r not in pair]
    came = cross + far + pair
    ncol = 8 * len(peer) + 4 * len(far) + 4 * len(cross)
    nmsg = 8 * (N - 1)

    V, S, E, Y = g.vector, g.scalar, g.tensor, g.sync
    Q = {"v": V, "s": S, "t": E, "p": g, "y": Y}
    cnt, seen = {}, {}

    def wait(q, deps):
        best = {}
        for s, v in deps:
            best[s] = max(best.get(s, 0), v)
        for s, v in best.items():
            if seen.get((q, s), 0) < v:
                Q[q].wait_ge(T.sem[s], v)
                seen[(q, s)] = v

    def do(q, call, *deps):
        wait(q, deps)
        name = "q" + q
        cnt[name] = cnt.get(name, 0) + 1
        call().then_inc(T.sem[name], 1)
        return (name, cnt[name])

    def load(q, sem, out, in_, *deps):
        wait(q, deps)
        cnt[sem] = cnt.get(sem, 0) + 16
        Q[q].dma_start(out, in_).then_inc(T.sem[sem], 16)
        return (sem, cnt[sem])

    def vset(ap, c, *deps):
        return do("v", lambda: V.memset(ap, c), *deps)

    def ts(out, in0, s1, s2, op0, op1, *deps):
        if op1 is None:
            return do("v", lambda: V.tensor_scalar(out, in0, s1, None, op0), *deps)
        return do("v", lambda: V.tensor_scalar(out, in0, s1, s2, op0, op1), *deps)

    def tt(out, a, b, op, *deps):
        return do("v", lambda: V.tensor_tensor(out, a, b, op), *deps)

    def vcopy(out, in_, *deps):
        return do("v", lambda: V.tensor_copy(out, in_), *deps)

    def red(out, in_, op, *deps):
        return do("v", lambda: V.tensor_reduce(out, in_, X, op), *deps)

    def scan(out, d0, d1, *deps, ops=(OP.mult, OP.add), init=0.0):
        return do("v", lambda: V.tensor_tensor_scan(out, d0, d1, init, *ops), *deps)

    def turn(out, in_, *deps):
        return do("v", lambda: V.transpose(out, in_), *deps)

    def act(out, in_, *deps):
        return do("s", lambda: S.activation(out, in_, COPY), *deps)

    def lin(out, in_, scale, bias, *deps, fn=None, sum_to=None):
        fn = fn or (COPY if isinstance(bias, float) else FN.Identity)
        return do("s", lambda: S.activation(out, in_, fn, bias, scale, accum_out=sum_to), *deps)

    def iota(ap, pattern, base, cm=0, flag=True):
        if flag:
            return do("p", lambda: g.iota(ap, pattern, base, cm, allow_small_or_imprecise_dtypes=True))
        return do("p", lambda: g.iota(ap, pattern, base, cm))

    def mm(out, n, q, s, a, b, *deps):
        return do("t", lambda: E.matmul_mx(out[:, 0:n], q[:, a:a + 128], s[:, a:a + 128], q[:, b:b + n], s[:, b:b + n], True, True), *deps)

    def count(k, tile, lead, out, *deps):
        q, s = T["q" + k], T["s" + k]
        return mm(out, 128, q, s, lead, 0, do("v", lambda: V.quantize_mx(q[:], s[:], tile[:]), *deps))

    def quad(t, a, *cols):
        return T[t][(slice(32 * a, 32 * a + 32),) + cols]

    def pickc(out, win, off, *deps):
        return do("v", lambda: V.tensor_copy(out.bitcast(dt.uint32), win.bitcast(dt.uint32).indirect(off)), *deps)

    def pick(dst, src, n, a, b, off, *deps):
        return (pickc(T[dst + "c"][:, a:b], T[src[0]][:, 0:n], off, *deps), act(T[dst + "s"][:, a:b], T[src[1]][:, 0:n].indirect(off), *deps))

    def send(tr, *deps):
        wait("p", deps)
        g.remote_dma_fused([t for t, n in tr], local_sem=T.sem.ls)
        cnt["ls"] = cnt.get("ls", 0) + sum(n for t, n in tr)

    def xfer(src, dsts, to, ab, sem):
        return (RemoteDMATransfer(dst_ids=[dest(topo, core, c) for c in to], dma_engine_mask=eng(topo, core, to[0], ab[0], ab[1]),
                                  remote_sem=T.sem[sem], srcs=[src], dsts=dsts), ab[1] - ab[0])

    def send_two(buf, rbuf, sem, *deps):
        send([xfer(view(T, buf, 64 * i, 64 * i + 64), [view(T, rbuf, 0, 64)], [r], HAND[i], sem) for i, r in enumerate(relays)], *deps)

    def send_four(buf, rbuf, sem, *deps):
        send([xfer(view(T, buf, 32 * i, 32 * i + 32), [view(T, rbuf, 32 * ap, 32 * ap + 32)], [relays_all[pair[i % 2]][i // 2]], (4 * i, 4 * i + 4), sem)
              for i in range(4)], *deps)

    def send_same(buf, land, sem, *deps):
        tr, at = [], 32 * me
        for i, r in enumerate(far + peer):
            a = 32 * pos.index(r)
            tr.append(xfer(view(T, buf, a, a + 32), [view(T, land, at, at + 32)], [T.cores[r]], COL["peer" if r in peer else i], sem))
        send(tr, *deps)

    def note_out(src, rbuf, sem, *deps):
        send([xfer(src, [T[rbuf][:]] * 2, relays, MSG["relay"], sem)], *deps)

    def note_same(src, land, sem, *deps):
        send([xfer(src, [seat(T, land, me, r) for r in to], [T.cores[r] for r in to], MSG[k], sem) for k, to in (("far", far), ("peer", peer))], *deps)

    ldp = load("y", "ldp", T.xh[:, 8:4 * AT], T.pl[:, 0:16])
    ldx = load("s", "ldx", T.xh[:, 4 * AT:536], T.x[:])
    ldw = load("y", "ldw", T.wh[:], T.w[:], ldx)
    i_d = iota(T.dd[:], [[1, 128]], 0, -1)
    i_8 = iota(T.i8[:], [[1, 8]], 0)
    i_p = iota(T.pb[:, 0:2], [[-AT, 2]], AT, 1, False)
    i_t = iota(T.pt[:], [[pos[k] - pos[0], 2] for k in (4, 2, 1)], pos[0])
    iota(T.pf[:, 0:1], [[1, 1]], 1, 2)
    i_f = iota(T.pf[:, 1:2], [[1, 1]], 127 - 32768, -1)
    i_r = iota(T.r2[:], [[0, 8], [256, 16], [4096, 2]], 32768)
    iota(T.kq[:], [[0, 8], [2 * (pos[4] - pos[0]), 2], [1, 2]], 0)
    i_v = iota(T.v16[:], [[1, 8], [128, 2], [0, 2]], 0)
    c_x = vset(T.xh[:, 0:8], 0.0)
    c_tx = vset(T.tx[:], 99.0)
    c_t2 = vset(T.t2x[:], 99.0)
    vset(T.t1[:, 34:544:4], 0.0)
    ts(T.tm[:, 0:128], T.dd[:], 0.0, 127.0 * 256, OP.is_equal, OP.mult, i_d)
    h = ts(T.tm[:, 128:256], T.dd[:], 0.0, 256.0, OP.is_ge, OP.mult)
    vset(T.kc[:, 8:16], 256.0 * (127 + CAPP))
    c_m = tt(T.t1[:, 32:544:4], T.tm[:, 0:128], T.tm[:, 128:256], OP.add, h)
    for k in (0, 3, 5):
        c_tx2 = act(T.tx[:, k:32:8], T.i8[:, 0:4], i_8, c_tx)
    act(T.m2[:, 0:256:2], T.t1[:, 32:544:4], c_m)
    c_m2 = lin(T.m2[:, 1:256:2], T.t1[:, 32:544:4], -1.0, 0.0)
    for k in (0, 3):
        c_t22 = act(T.t2x[:, k:32:4], T.pt[:], i_t, c_t2)
    c_f = lin(T.pf[:, 3:4], T.pf[:, 1:2], 1 / 128, 0.0, i_f)
    col = [T.pbh[:, i:i + 1] for i in range(10)]
    rho = col[5]

    xq = do("v", lambda: V.quantize_mx(T.xq[:], T.xs[:], T.xh[:]), ldx, ldp, c_x)
    z = mm(T.z, 134, T.xq, T.xs, AT, 0, xq)
    for k, c in enumerate((240, 15, 31)):
        h = ts(T.pb[:, 2 + 2 * k:4 + 2 * k], T.pb[:, 0:2], c, None, OP.bitwise_and, None, i_p)
    ts(T.dz[:], T.dd[:], 0.0, BIG, OP.not_equal, OP.mult)
    c_pb = vcopy(T.pbh[:, 0:8], T.pb[:], h)
    b0, b1, b2 = [T.bt[:, i:i + 1] for i in range(3)]
    h0 = ts(T.bt[:, 0:2], T.z[:, 2:4], 0.0, None, OP.is_lt, None, z)
    h1 = ts(b2, T.z[:, 4:5], 0.0, 2.0, OP.is_lt, OP.mult)
    ts(T.t1[:, 33:544:2], T.m2[:], b0, None, OP.mult, None, h0, c_m2)
    h = ts(T.t1[:, 0:32], T.tx[:], b1, b2, OP.subtract, OP.is_equal, h1, c_tx2)
    hb = ts(T.bk[:, 0:1], b1, b2, 2.0, OP.add, OP.mult)
    cn = count("1", T.t1, 8, T.cn, h)
    h = ts(T.bk[:, 1:2], T.bk[:, 0:1], b0, None, OP.add, None, hb)
    tt(T.pd[:, 0:128], T.z[:, AT:AT + 128], T.dz[:], OP.is_gt)
    hb = ts(T.sg[:, 1:2], T.bk[:, 1:2], 2.0 * CAPP, T.pf[:, 3:4], OP.mult, OP.add, h, c_f)
    hz = lin(T.junk[:, 0:128], T.pd[:, 0:128], T.pf[:, 0:1], T.sg[:, 1:2], hb, sum_to=T.sg[:, 0:1])
    for k in range(2):
        ts(T.t2[:, k:64:2], T.t2x[:], T.bk[:, 1:2], col[2 + 2 * k], OP.is_equal, OP.mult, c_t22)
    hv = scan(T.kc[:, 0:8], T.cn[:, 0:8], T.kc[:, 8:16], cn, ops=(OP.max, OP.min))
    h = red(T.key[:, 0:1], T.cn[:, 0:8], OP.max)
    ms = ts(T.ms[:, 0:1], T.kc[:, 7:8], T.sg[:, 0:1], None, OP.add, None, hv, hz)
    note_out(T.ms[:, 0:1], "rm1", "rn1", ms, i_v)
    send([xfer(T.ms[:, 0:1], [T.nlx[:, 4 + ap:5 + ap]], [T.cores[far[0]]], MSG["far"], "n1x"),
          xfer(T.ms[:, 0:1], [T.nl1[:, 8 * ap:8 * ap + 1]], [T.cores[peer[0]]], MSG["peer"], "n1")])
    for k in range(2):
        h2 = ts(T.t2[:, 64 + k:576:2], T.r2[:], T.key[:, 0:1], None, OP.is_equal, None, h, i_r)
    lp = count("2", T.t2, 16, T.lp, h2)
    ts(T.tri[:, 0:128], T.dd[:, 127::-1], 0.0, BIG, OP.is_lt, OP.mult)
    ts(T.dm[:], T.dd[:], 0.0, 0.9375, OP.is_equal, OP.mult)
    XQ, L1 = ("xq", "xs"), ("land1c", "land1s")
    o1 = vcopy(T.off1[:], T.lp[:, 0:16], lp)
    pk = [pick("slot1", XQ, 134, 128 * e, 128 * e + 128, T.off1[:, 8 * e:8 * e + 8], o1) for e in range(2)]
    send_four("slot1c", "r1c", "rc1", pk[0][0])
    send_four("slot1s", "r1s", "rs1", pk[0][1])
    send_same("slot1c", "land1c", "a1", pk[1][0])
    send_same("slot1s", "land1s", "a1", pk[1][1])
    i_1 = iota(T.r1[:], [[0, 8], [1, 16]], 0)
    if me == 0:
        i_1 = iota(T.nk[:, 0:32], [[128, 8], [0, 4]], 8192 - 128)
    a1, n1x = ("a1", 2 * ncol), ("n1x", 48 if ap == 0 else 16)
    if ap == 0:
        send([xfer(T.nlx[:], [T.nlx[:]], [T.cores[peer[0]]], (0, 16), "n1x")], n1x)
    i = pos.index(me)
    own1 = pick("land1", XQ, 134, 32 * me, 32 * me + 32, T.off1[:, 2 * i:2 * i + 2], o1)

    load("y", "ldz", T.land3c[:, 256:258].bitcast(dt.uint8), T.xq[:, 0:2].bitcast(dt.uint8), xq)
    ldz = load("y", "ldz", T.land3s[:, 256:258], T.xs[:, 0:2], xq)
    own_n = vcopy(T.nl1[:, 8 * ap:8 * ap + 1], T.ms[:, 0:1], ms)
    for k in range(2):
        for j in range(2):
            lin(T.kv[:, 16 * j + k:16 * j + 16:2], T.pt[:], 0.125, 256.0 + k / 16)
    for a in range(4):
        hk = lin(quad("kv", a, slice(32, 64)), quad("kq", a, slice(0, 32)), 1 / 16, 256.0 + pos[a] / 8, i_v)
    if me == 0:
        c_wa = vset(T.wa[:], 0.0)
    h = vset(T.c3[:], 0.0)
    vset(T.t3[:], 0.0)
    for b in range(2):
        h3 = vset(T.c3[:, 264 * b:264 * b + 8], BIG, h)
        ts(T.c3[:, 264 * b + 8:264 * b + 264:2], T.dd[:], 0.0, BIG, OP.is_lt, OP.mult)
    h = turn(T.kt[:], T.kv[:], hk)
    if me:
        vset(T.cl[:, 8 * me:8 * me + 1], -WHOLE)
        vset(T.cl[:, 8 * me + 8:8 * me + 9], WHOLE)
    vcopy(T.kk[:, 0:2], T.kt[:, 0:64:32], h)
    c_k = ts(T.kk[:, 2:4], T.kt[:, 0:64:32], -7.5 / 16, None, OP.add, None)
    for j in range(0, N, 2):
        i_c = lin(T.rf[:, 2 * came[j]:2 * came[j] + 4], T.v16[:, 0:4], 1 / 128, float(j))
    h5 = lin(T.rb[:], T.r2[:], 0.0, 0.0, i_r)
    lin(T.pf[:, 2:3], col[7], -256.0, -256.0 * CAPP * me - 128.0, c_pb)
    h6 = lin(T.nb[:], T.r2[:], 0.0, 0.0)
    lin(T.rb[:, 0:256:32], T.i8[:], 0.0, BIG, h5)
    lin(T.one[:], T.r2[:, 0:16], 0.0, 1.0)
    h5 = lin(T.rst9[:], T.r2[:, 0:72], 0.0, 1.0)
    lin(T.nb[:, 1:256:32], T.i8[:], 128.0, 0.0, h6)
    lin(col[8], col[3], 1.0, 128.0)
    h4 = lin(T.pf[:, 4:5], rho, 1.0, me / 8)
    lin(T.nft[:, 256:264], T.i8[:], 0.0, -1.0)
    lin(T.rst9[:, 0:72:9], T.i8[:], 0.0, 0.0, h5)
    lin(T.gg[:], T.i8[:], 16.0, T.pf[:, 4:5], h4)
    c_s = lin(T.it[:, 0:72:9], T.i8[:], 16.0, T.pf[:, 4:5])

    vcopy(T.nlf[:, 6:8], T.nl1[:, 0:16:8], ("n1", 8), own_n)
    if me == 0:
        ts(T.wa[:, 0:2], T.nl1[:, 0:16:8], 256.0, -1.0, OP.min, OP.mult, c_wa)
        for j in (4, 0, 2):
            h = ts(T.wa[:, came[j]:came[j] + 2], T.nlx[:, j:j + 2], 256.0, -1.0, OP.min, OP.mult, n1x)
    c_w = do("v", lambda: V.quantize_mx(T.wq[:], T.ws[:], T.wh[:]), ldw, i_1)
    if me == 0:
        h = turn(T.wb[:, 0:32], T.wa[:, 0:32], h)
        h = lin(T.junk[:, 0:32], T.wb[:, 0:32], 1.0, 0.0, h, sum_to=T.wa[:, 32:33])
    c_tri = vset(T.tri[:, 128:256], BIG)
    c_rep = vcopy(T.rep[:], T.rf[:], i_c)
    for k in (2, 5, 268):
        vset(T.c3[:, k:k + 1], 0.0, h3)
    if ap == 0:
        hn = vcopy(T.nlf[:, 0:6], T.nlx[:], n1x)
    if me == 0:
        h = turn(T.wb[:, 32:64], T.wa[:, 32:64], h)
        for a in range(4):
            h2 = act(T.wa[0:1, 64 + a:96:4], T.wb[32 * a:32 * a + 1, 32:40], h)
        w4 = do("p", lambda: g.partition_broadcast(T.wc[:], T.wa[0:1, 64:96], 128), h2, i_1)

    gs = [T.ga, T.gb]
    wd = [(slice(128 * b, 128 * b + 128), slice(128 * b, 128 + 256 * b), 128 + 128 * b) for b in range(2)]
    gm = [mm(gs[b], wd[b][2], T.land1c, T.land1s, 128 * b, 0, a1, *own1) for b in range(2)]
    mx, th = [], []
    for b in range(2):
        w, w2, n = wd[b]
        h = tt(T.pd[:, w], gs[b][:, w], T.dm[:], OP.mult, gm[b], hz)
        th.append(lin(T.junk[:, w], T.pd[:, w], 1.0, 0.0, h, sum_to=T.thr[:, b:b + 1]))
        mx.append(scan(T.xg[:, w2], gs[b][:, n - 1::-1], T.tri[:, 0:n], c_tri, ops=(OP.max, OP.min)))
        if ap and b == 0:
            hn = vcopy(T.nlf[:, 0:6], T.nlx[:], n1x)
    for b in range(2):
        at = 128 * b + wd[b][2] - 1
        t3 = ts(T.t3[:, b:512:4], T.c3[:, 528:656], T.xg[:, at:at + 1], T.thr[:, b:b + 1], OP.add, OP.is_lt, mx[b], th[b])
    rp = act(T.rp[:], T.nlf[:].indirect(T.rep[:]), hn, c_rep)
    sp = count("3", T.t3, 0, T.sp, t3)
    size, e8 = T.szb[:, 0:1], T.en[:, 96:97]

    def half(k):
        w = slice(128 * k, 128 * k + 128)
        return lin(T.ab[:, w], T.rt[:, w], 1.0, T.pf[:, 2:3], turn(T.rt[:, w], T.rp[:, w], rp), c_s, fn=FN.Abs)

    if me == 0:
        ts(T.en[:, 0:32], T.wc[:], -8192.0, None, OP.is_le, None, w4)
        h = ts(T.en[:, 32:64], T.wc[:], 128.0 - 8192, None, OP.is_gt, None)
    for b in range(2):
        t5 = ts(T.t5[:, b:528:2], T.c3[:, 264 * b:264 * b + 264], 0.5, T.t3[:, b:b + 1], OP.is_lt, OP.mult)
        if me == 0 and b == 0:
            he = scan(T.en[:, 64:96], T.en[:, 31::-1], T.en[:, 63:31:-1], h)
    if me == 0:
        sz = ts(size, T.sp[:, 0:1], T.en[:, 95:96], 0.125, OP.add, OP.mult, sp, he)
    ab = [half(0)]
    if me:
        sz = ts(size, T.sp[:, 0:1], 0.125, None, OP.mult, None, sp)

    send([xfer(size, [T.rm2[:]], [k], HAND[j], "rn2") for j, k in enumerate(relays)], sz)
    note_same(size, "cl", "c2")
    cu = count("5", T.t5, 4, T.cn, t5)
    ab.append(half(1))
    qd = ts(T.qd[:], T.t3[:, 0:2], -257.0, 256.0, OP.mult, OP.add)
    scan(T.sm[:, 0:128], T.rb[:, 0:128], T.ab[:, 0:128], ab[0], ops=(OP.add, OP.min))
    h = tt(T.ti[:], T.cn[:, 1:3], T.qd[:], OP.add, qd, cu)
    sm = scan(T.sm[:, 128:256], T.rb[:, 0:128], T.ab[:, 128:256], ab[1], ops=(OP.add, OP.min))
    hq = [act(T.mq[0:32, a:32:4], quad("sm", a, slice(31, 256, 32)), sm) for a in range(4)]
    ts(T.uv[:, 0:2], T.ti[:], 3, 15, OP.logical_shift_right, OP.bitwise_and, h)
    h = ts(T.uv[:, 2:4], T.ti[:], 256 + 128 + 7, None, OP.bitwise_and, None)
    if me == 0:
        he = ts(e8, T.en[:, 95:96], 0.125, None, OP.mult, None)
    h = vcopy(T.uvf[:], T.uv[:], h)
    for b in range(2):
        ts(T.t4[:, b:64:2], T.v16[:], T.uvf[:, 2 + b:3 + b], None, OP.is_equal, None, h)
        for k in range(2):
            h2 = ts(T.t4[:, 64 + b + 2 * k:576:4], T.r1[:], T.uvf[:, b:b + 1], rho if k else col[8 if b else 3], OP.is_equal, OP.mult)
    hm = scan(T.mr[0:32, :], T.rb[0:32, 0:256:8], T.mq[0:32, :], *hq, ops=(OP.add, OP.min))
    pp = count("4", T.t4, 16, T.pp, h2)
    for a in range(4):
        nb = act(quad("nb", a, slice(0, 256, 32)), T.mr[0:32, 3:32:4], hm)
    plw = act(T.plw[:], T.pp[:, 0:16], pp)

    c2 = ("c2", nmsg)
    if me:
        ov = []
        for k in range(2):
            for j, n in ((1, me + 2), (0, me)):
                h = scan(T.sq[:, 32 * k + 16 * j:32 * k + 16 * j + n], T.one[:, 0:n], T.cl[:, 0:8 * n:8], c2, c_k,
                         ops=(OP.mult, OP.subtract), init=T.kk[:, 2 * j + k:2 * j + k + 1])
            ov.append(h)
        done = h
        for k in range(2):
            ov[k] = ts(T.ov[:, 2 * k:2 * k + 1], T.sq[:, 32 * k + me - 1:32 * k + me], T.sq[:, 32 * k + me + 17:32 * k + me + 18], 16.0,
                       OP.subtract, OP.mult, ov[k])
            if k == 0:
                nj = turn(T.nj[:], T.nb[:], nb)
    else:
        ts(T.vi[:], T.kk[:, 2:4], e8, None, OP.subtract, None, he, c_k)
        done = h = ts(T.vx[:, 0:2], T.kk[:, 0:2], e8, None, OP.subtract, None)
        nj = turn(T.nj[:], T.nb[:], nb)
        ov = [ts(T.ov[:, 2 * k:2 * k + 1], T.vi[:, k:k + 1], T.vx[:, k:k + 1], -16.0, OP.subtract, OP.mult, h) for k in range(2)]
    o3 = vcopy(T.off3[:], T.plw[:].indirect(T.ov[:, 0:1]), ov[0], plw)
    on = vcopy(T.offn[:], T.plw[:].indirect(T.ov[:, 2:3]), ov[1])
    lin(T.cl[:, 8 * me:8 * me + 1], size, 0.0, 0.0, done)
    own_c = act(T.cl[:, 8 * me + 8:8 * me + 9], size)
    n3 = act(T.n3[:], T.nj[:].indirect(T.offn[:, 0:4]), on, nj)
    pc, ps = pick("slot3", L1, 256, 0, 128, T.off3[:, 0:8], o3, a1, *own1)
    send_two("slot3c", "r3c", "rc3", pc)
    send_four("slot3s", "r3s", "rs3", ps)
    pc, ps = pick("slot3", L1, 256, 128, 256, T.off3[:, 8:16], o3)
    h = turn(T.nt3[:], T.n3[:], n3)
    hc = pickc(T.land3c[:, 32 * me:32 * me + 32], T.land1c[:], T.off3[:, 2 * i:2 * i + 2])
    if me:
        end = scan(T.end[:], T.one[:, 0:9], T.cl[:, 0:72:8], own_c)
    m3 = [ts(T.m3[:, k:k + 1], T.nt3[:, 32 * k:32 * k + 1], T.nt3[:, 32 * k + 1:32 * k + 2], None, OP.add, None, h) for k in range(2)]
    own3 = (hc, act(T.land3s[:, 32 * me:32 * me + 32], T.land1s[:].indirect(T.off3[:, 2 * i:2 * i + 2])))
    note_out(T.m3[:, 0:1], "rm3", "rn3", m3[0])
    send_same("slot3c", "land3c", "a3", pc)
    send_same("slot3s", "land3s", "a3", ps)
    note_same(T.m3[:, 1:2], "nl3", "n3", m3[1])
    c_nf = lin(T.nf[:], T.r2[:], 0.0, 0.0)

    hd = ts(T.d256[:], T.cl[:, 0:72:8], -1.0, 32.0, OP.mult, OP.add, c2, own_c)
    if me == 0:
        end = scan(T.end[:], T.one[:, 0:9], T.cl[:, 0:72:8])
        ts(T.it[:, 0:72:9], T.gg[:], e8, None, OP.subtract, None)
    own_n3 = ts(T.nl3[:, 8 * me:8 * me + 1], T.nt3[:, 32:33], T.nt3[:, 33:34], None, OP.add, None)
    if me == 0:
        hd = ts(T.d256[:, 1:2], T.d256[:, 1:2], e8, None, OP.add, None, hd)
    for d in range(N)[::-1]:
        k = d + (d >= me)
        h2 = ts(T.it[:, 1 + d:72:9], T.gg[:], T.end[:, k:k + 1], T.d256[:, k:k + 1], OP.is_ge, OP.mult, end, *([hd] if me or d == 0 else []))
    if me == 0:
        nk = tt(T.nk[:, 32:64], T.wc[:], T.nk[:, 0:32], OP.add)
        ts(T.vx[:, 2:3], T.gg[:, 0:1], e8, 258.0, OP.is_lt, OP.mult)
    h = scan(T.its[:], T.rst9[:], T.it[:], h2)
    if me == 0:
        nk = tt(T.nk[:, 64:96], T.nk[:, 32:64], T.en[:, 32:64], OP.mult, nk)
    h = ts(T.xsh[:], T.its[:, 8:72:9], -0.4375, None, OP.add, None, h)
    if me == 0:
        nk = scan(T.nk[:, 96:128], T.en[:, 31::-1], T.nk[:, 95:63:-1], nk)
        ts(T.offz[:, 1:8], T.xsh[:, 1:8], 256.0, None, OP.min, None, h)
        oz = ts(T.offz[:, 0:1], T.xsh[:, 0:1], 256.0, T.vx[:, 2:3], OP.min, OP.add)
        ts(T.nft[:, 257:258], T.nk[:, 127:128], -1.0, None, OP.add, None, nk)
    else:
        oz = ts(T.offz[:], T.xsh[:], 256.0, None, OP.min, None, h)

    a3 = ("a3", 2 * ncol)
    fc = pickc(T.fq[:], T.land3c[:], T.offz[:], a3, ldz, oz, *own3)
    fs = act(T.fs[:], T.land3s[:].indirect(T.offz[:]), a3, ldz, oz, *own3)
    yp = do("t", lambda: E.matmul_mx(T.yp[:, 0:128], T.wq[:], T.ws[:], T.fq[:], T.fs[:], True, True), fc, fs, c_w)
    load("y", "dout", T.oc[:], T.fq[:].bitcast(dt.uint8), fc)
    h = vcopy(T.nf[:, 0:256:32], T.nl3[:, 0:64:8], ("n3", nmsg), own_n3, c_nf)
    h = turn(T.nft[:, 0:256], T.nf[:], h)
    for k in range(4):
        load("y", "dout", T.osc[4 * k:4 * k + 4, :], T.fs[32 * k:32 * k + 4, :], fs)
    ys = act(T.ysb[:], T.yp[:, 0:128], yp)
    load("y", "dout", T.y[:], T.ysb[:], ys)
    no = vcopy(T.no[:, 0:64], T.nft[:].indirect(T.offz[:, 0:4]), h), act(T.no[:, 64:128], T.nft[:].indirect(T.offz[:, 4:8]), h)
    load("y", "dout", T.num[:], T.no[32 * am:32 * am + 1, :], *no)
    wait("p", [(s, cnt[s]) for s in ("qv", "qs", "qt", "qp", "dout", "ls", "ldz", "ldp", "ldx", "ldw")])
